import numpy as np, ml_dtypes
CORES = [40,64,80,88,96,104,120,144]
N = 8
import mx_ref
BF = ml_dtypes.bfloat16
def pick(q, e):
    c = np.concatenate([q[0].reshape(128, -1, 4), np.zeros((128, 1, 4), np.uint8)], axis=1); s = np.concatenate([q[1], np.ones((16, 1), np.uint8)], axis=1)
    return (np.ascontiguousarray(c[:, e].reshape(128, -1)), np.ascontiguousarray(s[:, e]))
def join(*qs):
    return (np.concatenate([q[0] for q in qs], axis=1), np.concatenate([q[1] for q in qs], axis=1))
def put(q, e, v):
    c, s = q[0].reshape(128, -1, 4).copy(), q[1].copy(); c[:, e] = v[0].reshape(128, -1, 4); s[:, e] = v[1]
    return (c.reshape(128, -1), s)
def pk(c, s):
    return (np.ascontiguousarray(c), mx_ref.live(s))
def emit(q):
    return q[0], q[1]
def cut(t, i, w=512):
    return t[:, w * i:w * i + w]
def tile(rs):
    return np.stack(rs, axis=2).reshape(128, -1).astype(BF)
def f(rng, *shape):
    return mx_ref.flush((rng.standard_normal(shape, dtype=np.float32) * np.exp2(rng.integers(-2, 3, shape[:-1] + (1,)))).astype(BF))
def wide(rng, *shape, cols=0):
    v = rng.standard_normal(shape, dtype=np.float32) * np.exp2(rng.integers(-12, 13, shape)).astype(np.float32)
    if cols: v *= np.repeat(np.exp2(rng.integers(-cols, cols + 1, shape[:-2] + (1, shape[-1] // 4))) * (rng.random(shape[:-2] + (1, shape[-1] // 4)) > 0.0625), 4, axis=-1).astype(np.float32)
    return mx_ref.flush(v.astype(BF))
T, L, CAPP = 96, 3, 32
def game(x, u, w):
    S = [mx_ref.quantize(np.ascontiguousarray(x[r])) for r in range(N)]
    qu = [mx_ref.quantize(np.ascontiguousarray(u[r])) for r in range(N)]
    at, ks, made = np.arange(N * T).reshape(N, T), np.zeros((N, 1, L), np.float32), []
    for b in range(L):
        want = [np.flatnonzero(mx_ref.matmul(qu[r], S[r])[b] + np.float32(0) < 0) for r in range(N)]
        new, now = [], at.copy()
        for r in range(N):
            p = r ^ (1 << b)
            k = min(len(want[r]), len(want[p]), CAPP)
            to, of = want[r][:k], want[p][:k]
            c = pick(S[p], np.concatenate([of, np.full(CAPP - k, -1)]))
            t = tile([np.float32(0.0625) * mx_ref.matmul(mx_ref.quantize(np.ascontiguousarray(cut(w[r], 4 * b + i))), c) for i in range(4)])
            made.append(t)
            new.append(put(S[r], to, pick(mx_ref.quantize(t), np.arange(k))))
            now[r, to] = at[p, of]
            ks[r, 0, b] = k
        S, at = new, now
    return S, at, ks, made
def fit(t, low, high):
    a = np.abs(t.astype(np.float32))
    return bool((np.isfinite(a) & ((a == 0) | (a >= low) & (a <= high))).all())
def blocks(t):
    return np.abs(t.astype(np.float32)).reshape(16, 8, -1, 4).max(axis=(1, 3))
def plain(rng):
    u = np.array(f(rng, N, 128, 512))
    u[:, :, 4 * L:] = 0
    a = np.exp2(rng.integers(-2, 3, (N, 128, 1, 1)))
    x, lean = rng.standard_normal((N, 128, T, 4)), 2.5 * rng.random((N, L)) - 1
    for b in range(L):
        h = a * u[:, :, None, 4 * b:4 * b + 4].astype(np.float64)
        x += lean[:, b, None, None, None] * h * np.sum(h * h, axis=(1, 2, 3), keepdims=True) ** -0.5
    x = mx_ref.flush((a * x).reshape(N, 128, 4 * T).astype(np.float32).astype(BF))
    return {"x": x, "u": u, "w": f(rng, N, 128, 2048 * L), "v": f(rng, N, 128, 512)}
def aim(x, u, wish):
    x = x.reshape(N, 128, T, 4).astype(np.float32)
    for r in range(N):
        s = mx_ref.matmul(mx_ref.quantize(np.ascontiguousarray(u[r])), mx_ref.quantize(np.ascontiguousarray(x[r].reshape(128, 4 * T).astype(BF))))[0]
        x[r][:, s == 0] = u[r][:, None, :4].astype(np.float32)
        x[r][:, (s < 0) != wish[r]] *= -1
    return (x + np.float32(0)).reshape(N, 128, 4 * T).astype(BF)
def some(rng, n):
    return np.stack([rng.permutation(T) < n[r] for r in range(N)])
def setup_inputs(rng):
    return plain(rng)
def setup_inputs_many(rng):
    d = plain(rng)
    n = rng.integers(CAPP + 1, T + 1, N)
    j = 2 * int(rng.integers(0, N // 2))
    n[j:j + 2] = CAPP
    d["x"] = aim(d["x"], d["u"], some(rng, n))
    return d
def setup_inputs_none(rng):
    d = plain(rng)
    wish = some(rng, rng.integers(T // 4, T + 1, N))
    i, j = 2 * rng.permutation(N // 2)[:2] + rng.integers(0, 2, 2)
    wish[i] = False
    wish[i ^ 1] = True
    wish[j] = np.arange(T) == T - 1
    d["u"][int(rng.integers(0, N)), :, 4:8] = 0
    d["x"] = aim(d["x"], d["u"], wish)
    return d
def setup_inputs_zero(rng):
    d = plain(rng)
    d["u"][:, 64:, :4] = 0
    x = np.array(d["x"]).reshape(N, 128, T, 4)
    for r in range(N):
        e = rng.permutation(T)
        x[r][:, e[:T // 8]] = 0
        x[r][:64, e[T // 8:3 * T // 8]] = 0
    d["x"] = x.reshape(N, 128, 4 * T)
    return d
def setup_inputs_turn(rng):
    d = plain(rng)
    d["x"] = aim(d["x"], d["u"], some(rng, np.full(N, T // 2)))
    m, e = np.zeros((128, L, 4, 128, 4), np.float32), np.arange(128)
    for b in range(L):
        for i in range(4): m[e, b, i, e, i] = -16
    d["w"] = mx_ref.flush((m.reshape(128, 2048 * L) + d["w"].astype(np.float32) * np.float32(2.0 ** -6)).astype(BF))
    return d
def setup_inputs_spread(rng):
    d = plain(rng)
    u = np.array(wide(rng, N, 128, 512))
    u[:, :, 4 * L:] = 0
    return {**d, "x": wide(rng, N, 128, 4 * T, cols=6), "u": u, "v": wide(rng, N, 128, 512)}
def check_inputs(d):
    b = []
    for k in ("x", "u", "w", "v"):
        if not fit(d[k], 2.0 ** -30, 2.0 ** 30): b.append("a value of " + k)
    if (d["u"][:, :, 4 * L:].astype(np.float32) != 0).any(): b.append("u has numbers behind its first L columns")
    if not b:
        try:
            made = game(d["x"], d["u"], d["w"])[3]
            good, even = all(fit(t, 2.0 ** -60, 2.0 ** 60) for t in made), all(fit(blocks(t), 2.0 ** -30, 2.0 ** 30) for t in made)
        except Exception: good = even = False
        if not good: b.append("a number that an expert gives")
        if not even: b.append("the largest number of a block that an expert gives")
    return b
def reference(x, u, w, v):
    S, at, ks, made = game(x, u, w)
    oc, osc = np.zeros((N, 128, 4 * T), np.uint8), np.zeros((N, 16, T), np.uint8)
    y = np.zeros((N, 128, T), np.float32)
    for r in range(N):
        oc[r], osc[r] = emit(S[r])
        y[r] = mx_ref.matmul(mx_ref.quantize(np.ascontiguousarray(v[r])), S[r])
    return {"oc": oc, "osc": osc, "ids": at.reshape(N, 1, T).astype(np.float32), "ks": ks, "y": y}

@@ -1,0 +1,372 @@
+from concourse.bass import DstId, RemoteDMATransfer
+from concourse.mybir import dt, AluOpType, AxisListType, ActivationFunctionType
+
+PL, L, CAP = 96, 3, 32
+OP, AF = AluOpType, ActivationFunctionType
+F8, U8, F32, BF, U16, I32 = "float8_e4m3fn_x4", "uint8", "float32", "bfloat16", "uint16", "int32"
+BIG = 16384.0
+
+SCRATCH = {}
+
+
+def _buf(name, n, dtype, where="sbuf"):
+    SCRATCH[name] = (where, [128, n], dtype)
+
+
+def _pair(name, n):
+    _buf("q" + name, n, F8)
+    _buf("s" + name, n, U8)
+
+
+for _n, _w in (("xt", 512), ("ut", 512), ("vt", 512), ("wt0", 2048), ("wt1", 2048), ("wt2", 2048), ("h0", 512), ("h1", 512), ("h2", 512)):
+    _buf(_n, _w, BF)
+for _n, _w in (("a", 128), ("u", 128), ("g0", 128), ("g1", 128), ("g2", 128), ("w0", 512), ("w1", 512), ("w2", 512), ("v", 128),
+               ("b0", 224), ("b1", 128), ("b2", 128), ("f", 128), ("o0", 32), ("d0", 128), ("d1", 128), ("d2", 128), ("e1", 128), ("e2", 128)):
+    _pair(_n, _w)
+for _n in ("ps0", "ps1", "ps2", "pr0", "pr1", "pr2", "pr3", "pv"):
+    _buf(_n, 512, F32, "psum")
+for _n, _w in (("iot", 128), ("idf", 128), ("t16", 96), ("p6", 6), ("cc", 8), ("mk", 96), ("rs", 96), ("zz", 96), ("dd0", 12), ("dd1", 12),
+               ("so", 12), ("wn", 96), ("nw", 96), ("zc", 96), ("xk", 96), ("jk", 97), ("y0", 97), ("y1", 97), ("acc", 4), ("cw", 96),
+               ("dg", 96), ("ds", 96), ("e6", 6), ("t6", 6), ("lg1", 97), ("lg2", 97), ("dl", 96), ("si", 32), ("sit", 32), ("rb", 32),
+               ("iw0", 128), ("iw1", 128), ("iw2", 128), ("idl", 96), ("ksr", 3), ("ksb", 3), ("yb", 96)):
+    _buf(_n, _w, F32)
+_buf("iq", 2, I32)
+_buf("iqa", 2, I32)
+_buf("cf", 8 * L, U16)
+_buf("mo", 8 * L, U16)
+_buf("lo", 2 * L, U16)
+_buf("ll", 2 * L, U16)
+_buf("kk", L, BF)
+_buf("ko", L, BF)
+_buf("mine", L, U16)
+_buf("his", L, U16)
+for _n, _w in (("xw0", 16), ("xw1", 16), ("xu1", 64), ("xu2", 96), ("xc0", 32), ("xc1", 32), ("xc2", 32)):
+    _buf(_n, _w, F8)
+for _n, _w in (("xs0", 32), ("xs1", 128), ("xs2", 128)):
+    _buf(_n, _w, U8)
+_buf("xks", L, BF)
+_buf("xis", L, U16)
+_buf("xls", 2 * L, U16)
+
+FLOWS = {
+    "w0": (0, 1, "xw0", 0, "qd1", 0, 16), "w1": (1, 1, "xw1", 0, "qd1", 16, 16), "u1": (2, 1, "xu1", 0, "qd1", 32, 64), "u2": (2, 2, "xu2", 0, "qd2", 0, 96),
+    "c0": (0, 0, "xc0", 0, "qd0", 0, 32), "c1": (0, 1, "xc1", 0, "qd1", 96, 32), "c2": (0, 2, "xc2", 0, "qd2", 96, 32),
+    "s0": (1, 0, "xs0", 0, "sd0", 0, 32), "s1": (1, 1, "xs1", 0, "sd1", 0, 128), "s2": (1, 2, "xs2", 0, "sd2", 0, 128),
+    "k0": (1, 0, "xks", 0, "ko", 0, 1), "k1": (1, 1, "xks", 1, "ko", 1, 1), "k2": (1, 2, "xks", 2, "ko", 2, 1),
+    "l1": (0, 1, "xls", 2, "ll", 2, 2), "l2": (0, 2, "xls", 4, "ll", 4, 2),
+    "i0": (2, 0, "xis", 0, "his", 0, 1), "i1": (2, 1, "xis", 1, "his", 1, 1), "i2": (2, 2, "xis", 2, "his", 2, 1),
+}
+ORDER = (("w0", "c0", "c1", "l1", "c2", "l2"), ("w1", "s0", "k0", "s1", "k1", "s2", "k2"), ("u1", "i0", "u2", "i1", "i2"))
+
+SEMAPHORES = (["a_" + f for f in FLOWS] + ["sv", "ss", "st", "r0", "r1", "r2", "r3", "sg", "lsa", "lsb", "lx", "lu", "lw0", "lw1", "lw2", "lv",
+              "li0", "li1", "oy", "oc1", "oc2", "oi"])
+
+
+def _raw(view, name):
+    return view.bitcast(dt.uint8) if SCRATCH[name][2] == F8 else view
+
+
+def _mask(es):
+    return sum(1 << e for e in es)
+
+
+def _relays(core, T, topo):
+    r = T.rank_of(core)
+    ps = [T.cores[r ^ (1 << b)] for b in range(L)]
+    rel = [c for c in topo.cores_of(core) if c != core and all(topo.may_write(c, p) for p in ps)]
+    rel.sort(key=lambda c: (topo.die(c) != topo.die(core), c))
+    return rel[:3], ps
+
+
+def _hop1(f, src, dst, topo):
+    es = topo.engines(src, dst)
+    h = len(es) // 2
+    if f in ("w0", "c1", "c2"):
+        return es[:h]
+    if f in ("w1", "s1", "s2"):
+        return es[h:]
+    return es
+
+
+def _relay_program(g, core, me, partners, T, topo, rankcore):
+    sent = 0
+    for f in ORDER[me]:
+        _, lev, xb, xa, db, a, w = FLOWS[f]
+        g.wait_ge(T.sem["a_" + f], len(_hop1(f, rankcore, core, topo)))
+        dst = partners[lev]
+        rid, pid = topo.addr(dst, core)
+        es = topo.engines(core, dst)
+        g.remote_dma(_raw(T[db][:, a:a + w], db), _raw(T[xb][:, xa:xa + w], xb), T.sem["a_" + f], T.sem.lsa, pid, rid, _mask(es))
+        sent += len(es)
+    g.wait_ge(T.sem.lsa, sent)
+
+
+def rank_program(g, core, T, topo):
+    rank = T.rank_of(core)
+    if rank is None:
+        for rc in T.cores:
+            if rc in topo.cores_of(core):
+                rel, partners = _relays(rc, T, topo)
+                if core in rel:
+                    _relay_program(g, core, rel.index(core), partners, T, topo, rc)
+        return
+    rel, partners = _relays(core, T, topo)
+    cnt = {"sv": 0, "ss": 0, "lsa": 0, "lsb": 0}
+    seen = {}
+
+    def need(q, eng, toks):
+        for s, n in toks:
+            if seen.get((q, s), 0) < n:
+                eng.wait_ge(T.sem[s], n)
+                seen[(q, s)] = n
+
+    def bump(s, ins, n=1):
+        ins.then_inc(T.sem[s], n)
+        cnt[s] = cnt.get(s, 0) + n
+        return (s, cnt[s])
+
+    def run(q, eng, s, deps, call, args, kw):
+        need(q, eng, list(deps) + ([(s, cnt[s])] if cnt[s] else []))
+        return bump(s, call(*args, **kw))
+
+    def V(call, *args, deps=(), **kw):
+        return run("v", g.vector, "sv", deps, call, args, kw)
+
+    def S(*args, deps=(), **kw):
+        return run("s", g.scalar, "ss", deps, g.scalar.activation, args, kw)
+
+    def MM(s, out, lhs, rhs, deps):
+        need("t", g.tensor, deps)
+        return bump(s, g.tensor.matmul_mx(out, lhs[0], lhs[1], rhs[0], rhs[1], True, True))
+
+    def DMA(eng, q, s, out, in_, deps=()):
+        need(q, eng, deps)
+        return bump(s, eng.dma_start(out, in_), 16)
+
+    def codes(view):
+        return view.bitcast(dt.uint32)
+
+    def hop1(f, name, a, b):
+        k, _, xb, xa, _, _, w = FLOWS[f]
+        rid, pid = topo.addr(rel[k], core)
+        return rid, pid, _hop1(f, core, rel[k], topo), _raw(T[xb][:, xa:xa + w], xb), _raw(T[name][:, a:b], name)
+
+    def send(f, name, a, b, deps, ls="lsb"):
+        need("g", g, deps)
+        rid, pid, es, out, in_ = hop1(f, name, a, b)
+        g.remote_dma(out, in_, T.sem["a_" + f], T.sem[ls], pid, rid, _mask(es))
+        cnt[ls] += len(es)
+
+    def send2(parts, deps, ls="lsb"):
+        need("g", g, deps)
+        tr = []
+        for f, name, a, b in parts:
+            rid, pid, es, out, in_ = hop1(f, name, a, b)
+            tr.append(RemoteDMATransfer(dst_ids=[DstId(rid=rid, pnc=pid)], dma_engine_mask=_mask(es), remote_sem=T.sem["a_" + f], srcs=[in_], dsts=[out]))
+            cnt[ls] += len(es)
+        g.remote_dma_fused(tr, local_sem=T.sem[ls])
+
+    def arr(f):
+        src = _relays(partners[FLOWS[f][1]], T, topo)[0][FLOWS[f][0]]
+        return ("a_" + f, len(topo.engines(src, core)))
+
+    vec = g.vector
+    t_u = DMA(g.sync, "y", "lu", T.ut[:, 0:16], T.u[:, 0:16])
+    t_x = DMA(g.scalar, "s", "lx", T.xt[:, 0:4 * PL], T.x[:, 0:4 * PL])
+    t_w = [DMA(g.sync, "y", "lw0", T.wt0[:, :], T.w[:, 0:2048]), None, None]
+
+    def iota(buf, n, pattern, base, cm):
+        return bump("sg", g.iota(T[buf][:, 0:n], pattern, base, cm, allow_small_or_imprecise_dtypes=True))
+    bump("sg", g.iota(T.iq[:, 0:2], [[0, 2]], 0, 1))
+    iota("t16", 96, [[0, 6], [1, 16]], 0, 0)
+    iota("p6", 6, [[16, 6]], 0, 0)
+    iota("iot", 128, [[1, 128]], 0, 0)
+    iota("idf", 128, [[1, 128]], rank * PL, 0)
+    t_io = iota("iw0", 96, [[1, 96]], rank * PL, 0)
+
+    V(vec.memset, T.ut[:, 16:512], 0.0)
+    V(vec.memset, T.xt[:, 384:512], 0.0)
+    t_cf = None
+    for b in range(L):
+        t_cf = V(vec.memset, T.cf[:, 8 * b:8 * b + 8], b)
+    V(vec.memset, T.zz[:, :], 0.0)
+    V(vec.memset, T.y1[:, 96:97], -96.0)
+    V(vec.tensor_scalar, T.iqa[:, :], T.iq[:, :], 15, None, OP.bitwise_and, deps=[t_io])
+    ic, jb0, jt1 = T.cc[:, 0:1], T.cc[:, 1:2], T.cc[:, 2:3]
+    lo, hi = (T.cc[:, 3:4], T.cc[:, 4:5]), (T.cc[:, 5:6], T.cc[:, 6:7])
+    V(vec.tensor_copy, ic, T.iqa[:, 0:1])
+    V(vec.tensor_scalar, jb0, ic, 256.0, 128.0, OP.mult, OP.add)
+    t_jc = V(vec.tensor_scalar, jt1, ic, 256.0, 4096.0, OP.mult, OP.add)
+    t_qu = V(vec.quantize_mx, T.qu[:, :], T.su[:, :], T.ut[:, :], deps=[t_u])
+
+    def gauge(b):
+        off = T.cf[:, 8 * b:8 * b + 8]
+        s = S(T["sg%d" % b][:, 0:128], T.su[:, 0:128].indirect(off), AF.Copy, deps=[t_qu, t_cf])
+        v = V(vec.tensor_copy, codes(T["qg%d" % b][:, 0:128]), codes(T.qu[:, 0:128]).indirect(off))
+        return [s, v]
+    t_g = [gauge(0), None, None]
+    t_qa = V(vec.quantize_mx, T.qa[:, :], T.sa[:, :], T.xt[:, :], deps=[t_x])
+
+    def score(b, q, deps):
+        return MM("st", T["ps%d" % b][:, 0:128], (T["qg%d" % b][:, 0:128], T["sg%d" % b][:, 0:128]), (T["q" + q][:, 0:128], T["s" + q][:, 0:128]), t_g[b] + deps)
+
+    def nonwant(b, t_wn):
+        t = S(T.nw[:, :], T.wn[:, :], AF.Identity, bias=BIG, scale=-64.0, accum_out=T.acc[:, 2:3], deps=[t_wn])
+        return t, S(T.kk[:, b:b + 1], T.acc[:, 2:3], AF.Identity, bias=24576.0, scale=-1.0 / 64)
+
+    t_st = score(0, "a", [t_qa])
+    t_qb = V(vec.quantize_mx, T.qb0[:, 0:128], T.sb0[:, 0:128], T.xt[:, :])
+    send2([("w0", "qb0", 0, 16), ("w1", "qb0", 16, 32)], [t_qb], "lsa")
+    t_wn = V(vec.tensor_scalar, T.wn[:, :], T.ps0[:, 0:96], 0.0, 256.0, OP.is_lt, OP.mult, deps=[t_st])
+    t_zc = V(vec.tensor_tensor_scan, T.zc[:, :], T.wn[:, :], T.zz[:, :], 0.0, OP.add, OP.add)
+    t_ac = S(T.jk[:, 0:96], T.zc[:, :], AF.Sign, bias=jb0, scale=-1.0, accum_out=T.acc[:, 0:1], deps=[t_zc, t_jc])
+    V(vec.tensor_scalar, T.y1[:, 0:96], T.zc[:, :], jt1, 2.0, OP.is_le, OP.mult)
+    V(vec.tensor_reduce, T.acc[:, 1:2], T.y1[:, 0:97], AxisListType.X, OP.add)
+    t_lo = V(vec.tensor_scalar, T.lo[:, 0:2], T.acc[:, 0:2], 96.0, 0.5, OP.add, OP.mult, deps=[t_ac])
+    t_os = S(T.so0[:, 0:32], T.sa[:, 0:128].indirect(T.lo[:, 0:2]), AF.Copy, deps=[t_lo])
+    t_oq = V(vec.tensor_copy, codes(T.qo0[:, 0:32]), codes(T.qa[:, 0:128]).indirect(T.lo[:, 0:2]))
+    send("c0", "qo0", 0, 32, [t_oq], "lsa")
+    send("s0", "so0", 0, 32, [t_os], "lsa")
+    t_nw, t_kk = nonwant(0, t_wn)
+    send("k0", "kk", 0, 1, [t_kk], "lsa")
+    send("u1", "qb0", 32, 96, [t_qb])
+    DMA(g.sync, "y", "li0", T.qd0[:, 32:128].bitcast(dt.uint8), T.qa[:, 0:96].bitcast(dt.uint8), [t_qa, ("lsa", cnt["lsa"])])
+    t_i0 = DMA(g.sync, "y", "li0", T.sd0[:, 32:128], T.sa[:, 0:96])
+    for q in ("b1", "b2", "f"):
+        DMA(g.sync, "y", "li1", T["q" + q][:, 96:128].bitcast(dt.uint8), T.qa[:, 96:128].bitcast(dt.uint8))
+        t_i1 = DMA(g.sync, "y", "li1", T["s" + q][:, 96:128], T.sa[:, 96:128])
+    t_w[1] = DMA(g.sync, "y", "lw1", T.wt1[:, :], T.w[:, 2048:4096])
+    t_v = DMA(g.sync, "y", "lv", T.vt[:, :], T.v[:, :])
+
+    V(vec.memset, T.h0[:, 128:512], 0.0)
+    V(vec.tensor_scalar, T.mk[:, :], T.t16[:, :], ic, None, OP.is_equal)
+    V(vec.tensor_scalar, T.rs[:, :], T.t16[:, :], 0.0, None, OP.is_gt)
+    V(vec.memset, T.dd0[:, :], 0.0)
+    V(vec.tensor_scalar, T.dd1[:, 1:12:2], T.p6[:, :], ic, None, OP.add)
+    V(vec.tensor_tensor, T.cw[:, :], T.zc[:, :], T.nw[:, :], OP.add, deps=[t_nw])
+
+    def merge_prep():
+        V(vec.tensor_tensor, T.dg[:, :], T.cw[:, :], T.mk[:, :], OP.mult)
+        V(vec.tensor_tensor_scan, T.ds[:, :], T.rs[:, :], T.dg[:, :], 0.0, OP.mult, OP.add)
+        V(vec.tensor_scalar, T.t6[:, :], T.ds[:, 15:96:16], 256.0 * CAP, BIG, OP.is_gt, OP.mult)
+        V(vec.tensor_tensor, T.e6[:, :], T.ds[:, 15:96:16], T.t6[:, :], OP.add)
+        V(vec.tensor_scalar, T.t6[:, :], T.ds[:, 15:96:16], 1.0 / 256, PL - 1.0, OP.mult, OP.add)
+        V(vec.tensor_tensor, T.dd1[:, 0:12:2], T.t6[:, :], T.dd1[:, 1:12:2], OP.subtract)
+
+    def merge_list(b):
+        V(vec.tensor_scalar, T.dd0[:, 1:12:2], T.e6[:, :], T.ko[:, b:b + 1], None, OP.is_le, deps=[arr("k%d" % b)])
+        V(vec.tensor_tensor_scan, T.so[:, :], T.dd0[:, :], T.dd1[:, :], 0.0, OP.mult, OP.add)
+        return V(vec.tensor_copy, T.mo[:, 8 * b:8 * b + 6], T.so[:, 1:12:2])
+
+    def ids_send(b, win):
+        V(vec.tensor_copy, T.si[:, 0:32], T[win][:, 0:128].indirect(T.lo[:, 2 * b:2 * b + 2]))
+        V(vec.transpose, T.sit[:, :], T.si[:, :])
+        t = V(vec.tensor_copy, T.mine[:, b:b + 1], T.sit[:, 0:1])
+        send("i%d" % b, "mine", b, b + 1, [t])
+
+    def ids_take(b, out):
+        V(vec.tensor_copy, T.acc[:, 3:4], T.his[:, b:b + 1], deps=[arr("i%d" % b)])
+        V(vec.tensor_scalar, T.rb[:, :], T.zz[:, 0:32], T.acc[:, 3:4], None, OP.add)
+        V(vec.transpose, T["iw%d" % b][:, 96:128], T.rb[:, :])
+        return V(vec.tensor_copy, out, T["iw%d" % b][:, 0:128].indirect(T.mo[:, 8 * b:8 * b + 6]))
+
+    def count_out(b):
+        return V(vec.tensor_scalar, T.ksr[:, b:b + 1], T.kk[:, b:b + 1], T.ko[:, b:b + 1], 256.0 * CAP, OP.min, OP.min)
+
+    def quant_w(b):
+        return V(vec.quantize_mx, T["qw%d" % b][:, :], T["sw%d" % b][:, :], T["wt%d" % b][:, :], deps=[t_w[b]])
+
+    def expert(b, n, deps, between=None):
+        q = "d%d" % b
+        h = T["h%d" % b]
+        tr = []
+        for i in range(4):
+            tr.append(MM("r%d" % i, T["pr%d" % i][:, 0:128], (T["qw%d" % b][:, 128 * i:128 * i + 128], T["sw%d" % b][:, 128 * i:128 * i + 128]),
+                         (T["q" + q][:, 0:128], T["s" + q][:, 0:128]), deps))
+        S(h[:, 0:4 * n:4], T.pr0[:, 0:n], AF.Copy, scale=0.0625, deps=[tr[0]])
+        ts = S(h[:, 2:4 * n:4], T.pr2[:, 0:n], AF.Copy, scale=0.0625, deps=[tr[2]])
+        V(vec.tensor_scalar, h[:, 1:4 * n:4], T.pr1[:, 0:n], 0.0625, None, OP.mult, deps=[tr[1]])
+        res = between() if between else None
+        V(vec.tensor_scalar, h[:, 3:4 * n:4], T.pr3[:, 0:n], 0.0625, None, OP.mult, deps=[tr[3]])
+        return ts, res
+
+    def gather_L(b, deps):
+        return S(T["lg%d" % b][:, 1:97], T.iot[:, 0:128].indirect(T.mo[:, 8 * b - 8:8 * b - 2]), AF.Copy, deps=deps)
+
+    def merge(b, out, deps):
+        off = T.mo[:, 8 * b:8 * b + 6]
+        s = S(T["s" + out][:, 0:96], T["sb%d" % b][:, 0:128].indirect(off), AF.Copy, deps=deps)
+        v = V(vec.tensor_copy, codes(T["q" + out][:, 0:96]), codes(T["qb%d" % b][:, 0:128]).indirect(off), deps=deps)
+        return [s, v]
+
+    merge_prep()
+    t_w0 = quant_w(0)
+    t_g[1] = gauge(1)
+    t_g[2] = gauge(2)
+    ids_send(0, "idf")
+    for j in (0, 1):
+        V(vec.tensor_scalar, lo[j], ic, 256.0, 256.0 + 4096.0 * j, OP.mult, OP.add)
+        V(vec.tensor_scalar, hi[j], ic, 256.0, 511.0 + 4096.0 * j, OP.mult, OP.add)
+        V(vec.tensor_scalar, T["y%d" % j][:, 96:97], ic, -24321.0, -48801.0 - 389136.0 * j, OP.mult, OP.add)
+    V(vec.memset, T.lg1[:, 0:1], 0.0)
+    t_pre = V(vec.memset, T.lg2[:, 0:1], 0.0)
+
+    t_s, t_mo = expert(0, 32, [t_w0, t_i0, arr("c0"), arr("s0")], lambda: merge_list(0))
+    t_lg = gather_L(1, [t_mo, t_pre])
+    t_c = V(vec.quantize_mx, T.qb0[:, 96:224], T.sb0[:, 96:224], T.h0[:, :], deps=[t_s])
+    t_cs = t_c
+    send2([("c1", "qb0", 96, 128), ("s1", "sb0", 0, 128)], [t_c])
+
+    for b in (1, 2):
+        t_m = merge(b - 1, "b%d" % b, [t_c, t_cs, t_mo])
+        if b == 2:
+            t_lg = gather_L(2, [t_mo, t_pre])
+        t_st = score(b, "b%d" % b, t_m + [t_i1])
+        lg = T["lg%d" % b]
+        V(vec.tensor_tensor, T.dl[:, :], lg[:, 1:97], lg[:, 0:96], OP.subtract, deps=[t_lg])
+        t_wn = V(vec.tensor_scalar, T.wn[:, :], T["ps%d" % b][:, 0:96], 0.0, 256.0, OP.is_lt, OP.mult, deps=[t_st])
+        t_nw, t_kk = nonwant(b, t_wn)
+        V(vec.tensor_tensor_scan, T.zc[:, :], T.wn[:, :], T.dl[:, :], 0.0, OP.add, OP.add)
+        V(vec.tensor_tensor, T.xk[:, :], T.zc[:, :], T.nw[:, :], OP.add, deps=[t_nw])
+        t_y0 = V(vec.tensor_scalar, T.y0[:, 0:96], T.xk[:, :], hi[0], lo[0], OP.min, OP.max)
+        V(vec.tensor_scalar, T.y1[:, 0:96], T.xk[:, :], hi[1], lo[1], OP.min, OP.max)
+        t_ac = S(T.jk[:, 0:97], T.y0[:, 0:97], AF.Copy, accum_out=T.acc[:, 0:1], deps=[t_y0])
+        V(vec.tensor_reduce, T.acc[:, 1:2], T.y1[:, 0:97], AxisListType.X, OP.add)
+        t_lo = V(vec.tensor_scalar, T.lo[:, 2 * b:2 * b + 2], T.acc[:, 0:2], 127.0, 0.0, OP.min, OP.max, deps=[t_ac])
+        send("k%d" % b, "kk", b, b + 1, [t_kk])
+        send("l%d" % b, "lo", 2 * b, 2 * b + 2, [t_lo])
+        if b == 1:
+            send("u2", "qb1", 0, 96, t_m)
+            t_w[2] = DMA(g.sync, "y", "lw2", T.wt2[:, :], T.w[:, 4096:6144], [t_lo])
+        t_wq = quant_w(b)
+        V(vec.tensor_tensor, T.cw[:, :], T.xk[:, :], lg[:, 1:97], OP.subtract)
+        merge_prep()
+        ids_take(b - 1, T["iw%d" % b][:, 0:96])
+        ids_send(b, "iw%d" % (b - 1))
+        if b == 1:
+            t_qv = V(vec.quantize_mx, T.qv[:, :], T.sv[:, :], T.vt[:, :], deps=[t_v])
+        count_out(b - 1)
+        early = ["w0", "w1", "u1"] if b == 1 else ["u2"]
+        t_s, _ = expert(b, 128, [t_wq] + [arr(f) for f in early + ["c%d" % b, "s%d" % b]])
+        t_e = V(vec.quantize_mx, T["qe%d" % b][:, :], T["se%d" % b][:, :], T["h%d" % b][:, :], deps=[t_s])
+        t_mo = merge_list(b)
+        off = T.ll[:, 2 * b:2 * b + 2]
+        d = [t_e, t_i1, arr("l%d" % b)]
+        t_cs = S(T["sb%d" % b][:, 96:128], T["se%d" % b][:, 0:128].indirect(off), AF.Copy, deps=d)
+        t_c = V(vec.tensor_copy, codes(T["qb%d" % b][:, 96:128]), codes(T["qe%d" % b][:, 0:128]).indirect(off), deps=d)
+        if b == 1:
+            send2([("c2", "qb1", 96, 128), ("s2", "sb1", 0, 128)], [t_c, t_cs])
+
+    t_m = merge(2, "f", [t_c, t_cs, t_mo])
+    t_st = MM("st", T.pv[:, 0:128], (T.qv[:, 0:128], T.sv[:, 0:128]), (T.qf[:, 0:128], T.sf[:, 0:128]), [t_qv, t_i1] + t_m)
+    DMA(g.sync, "y", "oc1", T.oc[:, 0:4 * PL], T.qf[:, 0:96].bitcast(dt.uint8), [t_m[1]])
+    for k in range(4):
+        DMA(g.scalar, "s", "oc2", T.osc[4 * k:4 * k + 4, 0:PL], T.sf[32 * k:32 * k + 4, 0:96], [t_m[0]])
+    t_y = V(vec.tensor_copy, T.yb[:, :], T.pv[:, 0:96], deps=[t_st])
+    DMA(g.sync, "y", "oy", T.y[:, :], T.yb[:, :], [t_y])
+    t_id = ids_take(2, T.idl[:, :])
+    DMA(g.scalar, "s", "oi", T.ids[0:1, :], T.idl[0:1, :], [t_id])
+    count_out(2)
+    t_ks = V(vec.tensor_scalar, T.ksb[:, :], T.ksr[:, :], 1.0 / 256, None, OP.mult)
+    DMA(g.sync, "y", "oi", T.ks[0:1, :], T.ksb[0:1, :], [t_ks])
+    need("g", g, [(s, n) for s, n in cnt.items() if n] + [arr(f) for f in FLOWS])

@@ -25,10 +25,10 @@ for _n, _w in (("a", 128), ("u", 128), ("g0", 128), ("g1", 128), ("g2", 128), ("
     _pair(_n, _w)
 for _n in ("ps0", "ps1", "ps2", "pr0", "pr1", "pr2", "pr3", "pv"):
     _buf(_n, 512, F32, "psum")
-for _n, _w in (("iot", 128), ("idf", 128), ("t16", 96), ("p6", 6), ("cc", 8), ("mk", 96), ("rs", 96), ("zz", 96), ("dd0", 12), ("dd1", 12),
-               ("so", 12), ("wn", 96), ("nw", 96), ("zc", 96), ("xk", 96), ("jk", 97), ("y0", 97), ("y1", 97), ("acc", 4), ("cw", 96),
-               ("dg", 96), ("ds", 96), ("e6", 6), ("t6", 6), ("lg1", 97), ("lg2", 97), ("dl", 96), ("si", 32), ("sit", 32), ("rb", 32),
-               ("iw0", 128), ("iw1", 128), ("iw2", 128), ("idl", 96), ("ksr", 3), ("ksb", 3), ("yb", 96)):
+for _n, _w in (("iot", 128), ("idf", 128), ("idp", 128), ("t16", 96), ("p6", 6), ("cc", 8), ("mk", 96), ("rs", 96), ("zz", 96), ("dd0", 12), ("dd1", 12),
+               ("so", 12), ("wn", 96), ("nw", 96), ("nl", 96), ("zc", 96), ("xk", 96), ("jk", 97), ("jk2", 96), ("y0", 97), ("y1", 97), ("acc", 4), ("cw", 96),
+               ("dg", 96), ("ds", 96), ("t6", 6), ("lg", 96), ("si", 32), ("sit", 32), ("rc", 1), ("rb", 32),
+               ("iw0", 128), ("iw1", 128), ("iw2", 128), ("idl", 96), ("ksb", 3), ("yb", 96)):
     _buf(_n, _w, F32)
 _buf("iq", 2, I32)
 _buf("iqa", 2, I32)
@@ -56,9 +56,10 @@ FLOWS = {
     "l1": (0, 1, "xls", 2, "ll", 2, 2), "l2": (0, 2, "xls", 4, "ll", 4, 2),
     "i0": (2, 0, "xis", 0, "his", 0, 1), "i1": (2, 1, "xis", 1, "his", 1, 1), "i2": (2, 2, "xis", 2, "his", 2, 1),
 }
-ORDER = (("w0", "c0", "c1", "l1", "c2", "l2"), ("w1", "s0", "k0", "s1", "k1", "s2", "k2"), ("u1", "i0", "u2", "i1", "i2"))
+ORDER = (("w0", "c0", "c1", "l1", "c2", "l2"), ("w1", "s0", "k0", "s1", "k1", "s2", "k2"), ("u1", "i0", "i1", "u2", "i2"))
 
-SEMAPHORES = (["a_" + f for f in FLOWS] + ["sv", "ss", "st", "r0", "r1", "r2", "r3", "sg", "lsa", "lsb", "lx", "lu", "lw0", "lw1", "lw2", "lv",
+VCH, SCH = ["va", "vb", "vp", "vi", "vq", "vk", "vm", "vc"], ["s1", "s2"]
+SEMAPHORES = (["a_" + f for f in FLOWS] + VCH + SCH + ["st", "r0", "r1", "r2", "r3", "sg", "sq", "lsa", "lsb", "lx", "lu", "lw0", "lw1", "lw2", "lv",
               "li0", "li1", "oy", "oc1", "oc2", "oi"])
 
 
@@ -111,8 +112,9 @@ def rank_program(g, core, T, topo):
                     _relay_program(g, core, rel.index(core), partners, T, topo, rc)
         return
     rel, partners = _relays(core, T, topo)
-    cnt = {"sv": 0, "ss": 0, "lsa": 0, "lsb": 0}
+    cnt = {"lsa": 0, "lsb": 0}
     seen = {}
+    vec = g.vector
 
     def need(q, eng, toks):
         for s, n in toks:
@@ -125,26 +127,32 @@ def rank_program(g, core, T, topo):
         cnt[s] = cnt.get(s, 0) + n
         return (s, cnt[s])
 
-    def run(q, eng, s, deps, call, args, kw):
-        need(q, eng, list(deps) + ([(s, cnt[s])] if cnt[s] else []))
+    def now(*names):
+        return [(s, cnt[s]) for s in (names or VCH + SCH) if cnt.get(s)]
+
+    def V(ch, call, *args, deps=(), free=False, **kw):
+        s = "v" + ch
+        need("v", vec, list(deps) + ([] if free else now(s)))
         return bump(s, call(*args, **kw))
 
-    def V(call, *args, deps=(), **kw):
-        return run("v", g.vector, "sv", deps, call, args, kw)
+    def S(ch, *args, deps=(), **kw):
+        need("s", g.scalar, list(deps) + now(ch))
+        return bump(ch, g.scalar.activation(*args, **kw))
 
-    def S(*args, deps=(), **kw):
-        return run("s", g.scalar, "ss", deps, g.scalar.activation, args, kw)
-
-    def MM(s, out, lhs, rhs, deps):
+    def MM(s, out, l, r, deps):
         need("t", g.tensor, deps)
-        return bump(s, g.tensor.matmul_mx(out, lhs[0], lhs[1], rhs[0], rhs[1], True, True))
+        (ln, la), (rn, ra) = l, r
+        return bump(s, g.tensor.matmul_mx(out[:, 0:128], T["q" + ln][:, la:la + 128], T["s" + ln][:, la:la + 128],
+                                          T["q" + rn][:, ra:ra + 128], T["s" + rn][:, ra:ra + 128], True, True))
 
     def DMA(eng, q, s, out, in_, deps=()):
         need(q, eng, deps)
         return bump(s, eng.dma_start(out, in_), 16)
 
-    def codes(view):
-        return view.bitcast(dt.uint32)
+    def pick(ch, out, a, win, n, off, w, deps=()):
+        s = S("s1", T["s" + out][:, a:a + w], T["s" + win][:, 0:n].indirect(off), AF.Copy, deps=deps)
+        v = V(ch, vec.tensor_copy, T["q" + out][:, a:a + w].bitcast(dt.uint32), T["q" + win][:, 0:n].bitcast(dt.uint32).indirect(off), deps=deps)
+        return [v, s]
 
     def hop1(f, name, a, b):
         k, _, xb, xa, _, _, w = FLOWS[f]
@@ -170,66 +178,65 @@ def rank_program(g, core, T, topo):
         src = _relays(partners[FLOWS[f][1]], T, topo)[0][FLOWS[f][0]]
         return ("a_" + f, len(topo.engines(src, core)))
 
-    vec = g.vector
+    def together(*chains):
+        for k in range(max(len(c) for c in chains)):
+            for c in chains:
+                if k < len(c) and c[k]:
+                    c[k]()
+
     t_u = DMA(g.sync, "y", "lu", T.ut[:, 0:16], T.u[:, 0:16])
     t_x = DMA(g.scalar, "s", "lx", T.xt[:, 0:4 * PL], T.x[:, 0:4 * PL])
     t_w = [DMA(g.sync, "y", "lw0", T.wt0[:, :], T.w[:, 0:2048]), None, None]
 
     def iota(buf, n, pattern, base, cm):
         return bump("sg", g.iota(T[buf][:, 0:n], pattern, base, cm, allow_small_or_imprecise_dtypes=True))
-    bump("sg", g.iota(T.iq[:, 0:2], [[0, 2]], 0, 1))
+    t_iq = bump("sq", g.iota(T.iq[:, 0:2], [[0, 2]], 0, 1))
     iota("t16", 96, [[0, 6], [1, 16]], 0, 0)
     iota("p6", 6, [[16, 6]], 0, 0)
     iota("iot", 128, [[1, 128]], 0, 0)
     iota("idf", 128, [[1, 128]], rank * PL, 0)
+    iota("idp", 128, [[1, 128]], T.rank_of(partners[1]) * PL, 0)
     t_io = iota("iw0", 96, [[1, 96]], rank * PL, 0)
 
-    V(vec.memset, T.ut[:, 16:512], 0.0)
-    V(vec.memset, T.xt[:, 384:512], 0.0)
-    t_cf = None
+    V("k", vec.memset, T.ut[:, 16:512], 0.0, free=True)
+    V("k", vec.memset, T.xt[:, 384:512], 0.0, free=True)
     for b in range(L):
-        t_cf = V(vec.memset, T.cf[:, 8 * b:8 * b + 8], b)
-    V(vec.memset, T.zz[:, :], 0.0)
-    V(vec.memset, T.y1[:, 96:97], -96.0)
-    V(vec.tensor_scalar, T.iqa[:, :], T.iq[:, :], 15, None, OP.bitwise_and, deps=[t_io])
-    ic, jb0, jt1 = T.cc[:, 0:1], T.cc[:, 1:2], T.cc[:, 2:3]
+        V("k", vec.memset, T.cf[:, 8 * b:8 * b + 8], b, free=True)
+    V("k", vec.memset, T.dd0[:, :], 0.0, free=True)
+    V("k", vec.memset, T.h0[:, 128:512], 0.0, free=True)
+    V("k", vec.memset, T.zz[:, :], 0.0, free=True)
+    t_k = now("vk")
+    ic, jb0, jb1 = T.cc[:, 0:1], T.cc[:, 1:2], T.cc[:, 2:3]
     lo, hi = (T.cc[:, 3:4], T.cc[:, 4:5]), (T.cc[:, 5:6], T.cc[:, 6:7])
-    V(vec.tensor_copy, ic, T.iqa[:, 0:1])
-    V(vec.tensor_scalar, jb0, ic, 256.0, 128.0, OP.mult, OP.add)
-    t_jc = V(vec.tensor_scalar, jt1, ic, 256.0, 4096.0, OP.mult, OP.add)
-    t_qu = V(vec.quantize_mx, T.qu[:, :], T.su[:, :], T.ut[:, :], deps=[t_u])
+    V("c", vec.tensor_scalar, T.iqa[:, :], T.iq[:, :], 15, None, OP.bitwise_and, deps=[t_iq])
+    V("c", vec.tensor_copy, ic, T.iqa[:, 0:1])
+    V("c", vec.tensor_scalar, jb0, ic, 256.0, 128.0, OP.mult, OP.add)
+    t_jc = V("c", vec.tensor_scalar, jb1, ic, 256.0, 4224.0, OP.mult, OP.add)
+    t_qu = V("a", vec.quantize_mx, T.qu[:, :], T.su[:, :], T.ut[:, :], deps=[t_u] + t_k)
 
-    def gauge(b):
-        off = T.cf[:, 8 * b:8 * b + 8]
-        s = S(T["sg%d" % b][:, 0:128], T.su[:, 0:128].indirect(off), AF.Copy, deps=[t_qu, t_cf])
-        v = V(vec.tensor_copy, codes(T["qg%d" % b][:, 0:128]), codes(T.qu[:, 0:128]).indirect(off))
-        return [s, v]
-    t_g = [gauge(0), None, None]
-    t_qa = V(vec.quantize_mx, T.qa[:, :], T.sa[:, :], T.xt[:, :], deps=[t_x])
+    def gauge(b, ch):
+        return pick(ch, "g%d" % b, 0, "u", 128, T.cf[:, 8 * b:8 * b + 8], 128, [t_qu] + t_k)
+    t_g = [gauge(0, "a"), None, None]
+    t_qb = V("b", vec.quantize_mx, T.qb0[:, 0:128], T.sb0[:, 0:128], T.xt[:, :], deps=[t_x])
+    send("u1", "qb0", 32, 96, [t_qb])
+    send2([("w0", "qb0", 0, 16), ("w1", "qb0", 16, 32)], [t_qb])
 
     def score(b, q, deps):
-        return MM("st", T["ps%d" % b][:, 0:128], (T["qg%d" % b][:, 0:128], T["sg%d" % b][:, 0:128]), (T["q" + q][:, 0:128], T["s" + q][:, 0:128]), t_g[b] + deps)
+        return MM("st", T["ps%d" % b], ("g%d" % b, 0), (q, 0), t_g[b] + deps)
 
-    def nonwant(b, t_wn):
-        t = S(T.nw[:, :], T.wn[:, :], AF.Identity, bias=BIG, scale=-64.0, accum_out=T.acc[:, 2:3], deps=[t_wn])
-        return t, S(T.kk[:, b:b + 1], T.acc[:, 2:3], AF.Identity, bias=24576.0, scale=-1.0 / 64)
-
-    t_st = score(0, "a", [t_qa])
-    t_qb = V(vec.quantize_mx, T.qb0[:, 0:128], T.sb0[:, 0:128], T.xt[:, :])
-    send2([("w0", "qb0", 0, 16), ("w1", "qb0", 16, 32)], [t_qb], "lsa")
-    t_wn = V(vec.tensor_scalar, T.wn[:, :], T.ps0[:, 0:96], 0.0, 256.0, OP.is_lt, OP.mult, deps=[t_st])
-    t_zc = V(vec.tensor_tensor_scan, T.zc[:, :], T.wn[:, :], T.zz[:, :], 0.0, OP.add, OP.add)
-    t_ac = S(T.jk[:, 0:96], T.zc[:, :], AF.Sign, bias=jb0, scale=-1.0, accum_out=T.acc[:, 0:1], deps=[t_zc, t_jc])
-    V(vec.tensor_scalar, T.y1[:, 0:96], T.zc[:, :], jt1, 2.0, OP.is_le, OP.mult)
-    V(vec.tensor_reduce, T.acc[:, 1:2], T.y1[:, 0:97], AxisListType.X, OP.add)
-    t_lo = V(vec.tensor_scalar, T.lo[:, 0:2], T.acc[:, 0:2], 96.0, 0.5, OP.add, OP.mult, deps=[t_ac])
-    t_os = S(T.so0[:, 0:32], T.sa[:, 0:128].indirect(T.lo[:, 0:2]), AF.Copy, deps=[t_lo])
-    t_oq = V(vec.tensor_copy, codes(T.qo0[:, 0:32]), codes(T.qa[:, 0:128]).indirect(T.lo[:, 0:2]))
-    send("c0", "qo0", 0, 32, [t_oq], "lsa")
-    send("s0", "so0", 0, 32, [t_os], "lsa")
-    t_nw, t_kk = nonwant(0, t_wn)
-    send("k0", "kk", 0, 1, [t_kk], "lsa")
-    send("u1", "qb0", 32, 96, [t_qb])
+    t_st = score(0, "b0", [t_qb])
+    t_qa = V("q", vec.quantize_mx, T.qa[:, :], T.sa[:, :], T.xt[:, :])
+    V("a", vec.tensor_scalar, T.wn[:, :], T.ps0[:, 0:96], 0.0, 256.0, OP.is_lt, OP.mult, deps=[t_st])
+    V("b", vec.tensor_scalar, T.nw[:, :], T.ps0[:, 0:96], 0.0, BIG, OP.is_ge, OP.mult)
+    t_zc = V("a", vec.tensor_tensor_scan, T.zc[:, :], T.wn[:, :], T.zz[:, :], 0.0, OP.add, OP.add)
+    t_a0 = S("s1", T.jk[:, 0:96], T.zc[:, :], AF.Sign, bias=jb0, scale=-1.0, accum_out=T.acc[:, 0:1], deps=[t_zc, t_jc])
+    t_a1 = S("s2", T.jk2[:, 0:96], T.zc[:, :], AF.Sign, bias=jb1, scale=-1.0, accum_out=T.acc[:, 1:2])
+    t_k0 = V("b", vec.tensor_scalar, T.kk[:, 0:1], T.zc[:, 95:96], 256.0 * CAP, None, OP.min, deps=[t_zc])
+    t_lo = V("a", vec.tensor_scalar, T.lo[:, 0:2], T.acc[:, 0:2], 96.0, 0.5, OP.add, OP.mult, deps=[t_a0, t_a1])
+    t_o = pick("a", "o0", 0, "a", 128, T.lo[:, 0:2], 32, [t_lo, t_qa])
+    send("c0", "qo0", 0, 32, t_o[:1], "lsa")
+    send("s0", "so0", 0, 32, t_o[1:], "lsa")
+    send("k0", "kk", 0, 1, [t_k0], "lsa")
     DMA(g.sync, "y", "li0", T.qd0[:, 32:128].bitcast(dt.uint8), T.qa[:, 0:96].bitcast(dt.uint8), [t_qa, ("lsa", cnt["lsa"])])
     t_i0 = DMA(g.sync, "y", "li0", T.sd0[:, 32:128], T.sa[:, 0:96])
     for q in ("b1", "b2", "f"):
@@ -238,135 +245,139 @@ def rank_program(g, core, T, topo):
     t_w[1] = DMA(g.sync, "y", "lw1", T.wt1[:, :], T.w[:, 2048:4096])
     t_v = DMA(g.sync, "y", "lv", T.vt[:, :], T.v[:, :])
 
-    V(vec.memset, T.h0[:, 128:512], 0.0)
-    V(vec.tensor_scalar, T.mk[:, :], T.t16[:, :], ic, None, OP.is_equal)
-    V(vec.tensor_scalar, T.rs[:, :], T.t16[:, :], 0.0, None, OP.is_gt)
-    V(vec.memset, T.dd0[:, :], 0.0)
-    V(vec.tensor_scalar, T.dd1[:, 1:12:2], T.p6[:, :], ic, None, OP.add)
-    V(vec.tensor_tensor, T.cw[:, :], T.zc[:, :], T.nw[:, :], OP.add, deps=[t_nw])
-
-    def merge_prep():
-        V(vec.tensor_tensor, T.dg[:, :], T.cw[:, :], T.mk[:, :], OP.mult)
-        V(vec.tensor_tensor_scan, T.ds[:, :], T.rs[:, :], T.dg[:, :], 0.0, OP.mult, OP.add)
-        V(vec.tensor_scalar, T.t6[:, :], T.ds[:, 15:96:16], 256.0 * CAP, BIG, OP.is_gt, OP.mult)
-        V(vec.tensor_tensor, T.e6[:, :], T.ds[:, 15:96:16], T.t6[:, :], OP.add)
-        V(vec.tensor_scalar, T.t6[:, :], T.ds[:, 15:96:16], 1.0 / 256, PL - 1.0, OP.mult, OP.add)
-        V(vec.tensor_tensor, T.dd1[:, 0:12:2], T.t6[:, :], T.dd1[:, 1:12:2], OP.subtract)
+    def prep(b):
+        def t6():
+            S("s2", T.t6[:, :], T.ds[:, 15:96:16], AF.Identity, bias=PL - 1.0, scale=1.0 / 256, deps=now("vp"))
+        return [lambda: V("p", vec.tensor_tensor, T.cw[:, :], T.zc[:, :], T.nw[:, :], OP.add, deps=now("va", "vb")),
+                lambda: V("p", vec.tensor_tensor, T.dg[:, :], T.cw[:, :], T.mk[:, :], OP.mult),
+                lambda: V("p", vec.tensor_tensor_scan, T.ds[:, :], T.rs[:, :], T.dg[:, :], 0.0, OP.mult, OP.add),
+                t6,
+                lambda: V("p", vec.tensor_tensor, T.dd1[:, 0:12:2], T.t6[:, :], T.dd1[:, 1:12:2], OP.subtract, deps=now("s2"))]
 
     def merge_list(b):
-        V(vec.tensor_scalar, T.dd0[:, 1:12:2], T.e6[:, :], T.ko[:, b:b + 1], None, OP.is_le, deps=[arr("k%d" % b)])
-        V(vec.tensor_tensor_scan, T.so[:, :], T.dd0[:, :], T.dd1[:, :], 0.0, OP.mult, OP.add)
-        return V(vec.tensor_copy, T.mo[:, 8 * b:8 * b + 6], T.so[:, 1:12:2])
+        return [lambda: V("m", vec.tensor_scalar, T.dd0[:, 1:12:2], T.ds[:, 15:96:16], T.ko[:, b:b + 1], None, OP.is_le, deps=[arr("k%d" % b)] + now("vp")),
+                lambda: V("m", vec.tensor_tensor_scan, T.so[:, :], T.dd0[:, :], T.dd1[:, :], 0.0, OP.mult, OP.add),
+                lambda: V("m", vec.tensor_copy, T.mo[:, 8 * b:8 * b + 6], T.so[:, 1:12:2])]
+
+    def mo(b):
+        return T.mo[:, 8 * b:8 * b + 6]
 
     def ids_send(b, win):
-        V(vec.tensor_copy, T.si[:, 0:32], T[win][:, 0:128].indirect(T.lo[:, 2 * b:2 * b + 2]))
-        V(vec.transpose, T.sit[:, :], T.si[:, :])
-        t = V(vec.tensor_copy, T.mine[:, b:b + 1], T.sit[:, 0:1])
-        send("i%d" % b, "mine", b, b + 1, [t])
+        def last():
+            t = V("i", vec.tensor_copy, T.mine[:, b:b + 1], T.sit[:, 0:1])
+            send("i%d" % b, "mine", b, b + 1, [t])
+        return [lambda: V("i", vec.tensor_copy, T.si[:, 0:32], T[win][:, 0:128].indirect(T.lo[:, 2 * b:2 * b + 2]), deps=now("va")),
+                lambda: V("i", vec.transpose, T.sit[:, :], T.si[:, :]), last]
 
     def ids_take(b, out):
-        V(vec.tensor_copy, T.acc[:, 3:4], T.his[:, b:b + 1], deps=[arr("i%d" % b)])
-        V(vec.tensor_scalar, T.rb[:, :], T.zz[:, 0:32], T.acc[:, 3:4], None, OP.add)
-        V(vec.transpose, T["iw%d" % b][:, 96:128], T.rb[:, :])
-        return V(vec.tensor_copy, out, T["iw%d" % b][:, 0:128].indirect(T.mo[:, 8 * b:8 * b + 6]))
+        return [lambda: V("i", vec.tensor_copy, T.rc[:, :], T.his[:, b:b + 1], deps=[arr("i%d" % b)]),
+                lambda: V("i", vec.tensor_scalar, T.rb[:, :], T.zz[:, 0:32], T.rc[:, 0:1], None, OP.add),
+                lambda: V("i", vec.transpose, T[out][:, 96:128], T.rb[:, :])]
 
-    def count_out(b):
-        return V(vec.tensor_scalar, T.ksr[:, b:b + 1], T.kk[:, b:b + 1], T.ko[:, b:b + 1], 256.0 * CAP, OP.min, OP.min)
+    def ids_pick(out, a, w, win, off, deps):
+        return V("i", vec.tensor_copy, T[out][:, a:a + w], T[win][:, 0:128].indirect(off), deps=deps)
 
     def quant_w(b):
-        return V(vec.quantize_mx, T["qw%d" % b][:, :], T["sw%d" % b][:, :], T["wt%d" % b][:, :], deps=[t_w[b]])
+        return V("q", vec.quantize_mx, T["qw%d" % b][:, :], T["sw%d" % b][:, :], T["wt%d" % b][:, :], deps=[t_w[b]])
 
-    def expert(b, n, deps, between=None):
-        q = "d%d" % b
+    def expert(b, n, deps, between):
         h = T["h%d" % b]
-        tr = []
-        for i in range(4):
-            tr.append(MM("r%d" % i, T["pr%d" % i][:, 0:128], (T["qw%d" % b][:, 128 * i:128 * i + 128], T["sw%d" % b][:, 128 * i:128 * i + 128]),
-                         (T["q" + q][:, 0:128], T["s" + q][:, 0:128]), deps))
-        S(h[:, 0:4 * n:4], T.pr0[:, 0:n], AF.Copy, scale=0.0625, deps=[tr[0]])
-        ts = S(h[:, 2:4 * n:4], T.pr2[:, 0:n], AF.Copy, scale=0.0625, deps=[tr[2]])
-        V(vec.tensor_scalar, h[:, 1:4 * n:4], T.pr1[:, 0:n], 0.0625, None, OP.mult, deps=[tr[1]])
-        res = between() if between else None
-        V(vec.tensor_scalar, h[:, 3:4 * n:4], T.pr3[:, 0:n], 0.0625, None, OP.mult, deps=[tr[3]])
-        return ts, res
+        tr = [MM("r%d" % i, T["pr%d" % i], ("w%d" % b, 128 * i), ("d%d" % b, 0), deps) for i in range(4)]
+        t0 = S("s1", h[:, 0:4 * n:4], T.pr0[:, 0:n], AF.Copy, scale=0.0625, deps=[tr[0]])
+        t2 = S("s2", h[:, 2:4 * n:4], T.pr2[:, 0:n], AF.Copy, scale=0.0625, deps=[tr[2]])
+        t1 = V("a", vec.tensor_scalar, h[:, 1:4 * n:4], T.pr1[:, 0:n], 0.0625, None, OP.mult, deps=[tr[1]])
+        if between:
+            between[0]()
+        t3 = V("b", vec.tensor_scalar, h[:, 3:4 * n:4], T.pr3[:, 0:n], 0.0625, None, OP.mult, deps=[tr[3]])
+        if between:
+            between[1]()
+        return [t0, t1, t2, t3]
 
-    def gather_L(b, deps):
-        return S(T["lg%d" % b][:, 1:97], T.iot[:, 0:128].indirect(T.mo[:, 8 * b - 8:8 * b - 2]), AF.Copy, deps=deps)
-
-    def merge(b, out, deps):
-        off = T.mo[:, 8 * b:8 * b + 6]
-        s = S(T["s" + out][:, 0:96], T["sb%d" % b][:, 0:128].indirect(off), AF.Copy, deps=deps)
-        v = V(vec.tensor_copy, codes(T["q" + out][:, 0:96]), codes(T["qb%d" % b][:, 0:128]).indirect(off), deps=deps)
-        return [s, v]
-
-    merge_prep()
-    t_w0 = quant_w(0)
-    t_g[1] = gauge(1)
-    t_g[2] = gauge(2)
-    ids_send(0, "idf")
+    need("v", vec, [t_io])
+    V("c", vec.tensor_scalar, T.mk[:, :], T.t16[:, :], ic, None, OP.is_equal, free=True)
+    V("c", vec.tensor_scalar, T.rs[:, :], T.t16[:, :], 0.0, None, OP.is_gt, free=True)
+    V("c", vec.tensor_scalar, T.dd1[:, 1:12:2], T.p6[:, :], ic, None, OP.add, free=True)
     for j in (0, 1):
-        V(vec.tensor_scalar, lo[j], ic, 256.0, 256.0 + 4096.0 * j, OP.mult, OP.add)
-        V(vec.tensor_scalar, hi[j], ic, 256.0, 511.0 + 4096.0 * j, OP.mult, OP.add)
-        V(vec.tensor_scalar, T["y%d" % j][:, 96:97], ic, -24321.0, -48801.0 - 389136.0 * j, OP.mult, OP.add)
-    V(vec.memset, T.lg1[:, 0:1], 0.0)
-    t_pre = V(vec.memset, T.lg2[:, 0:1], 0.0)
+        V("c", vec.tensor_scalar, lo[j], ic, 256.0, 256.0 + 4096.0 * j, OP.mult, OP.add, free=True)
+        V("c", vec.tensor_scalar, hi[j], ic, 256.0, 511.0 + 4096.0 * j, OP.mult, OP.add, free=True)
+        V("c", vec.tensor_scalar, T["y%d" % j][:, 96:97], ic, -24321.0, -48801.0 - 389136.0 * j, OP.mult, OP.add, free=True)
+    need("v", vec, now("vc"))
+    t_ws = []
 
-    t_s, t_mo = expert(0, 32, [t_w0, t_i0, arr("c0"), arr("s0")], lambda: merge_list(0))
-    t_lg = gather_L(1, [t_mo, t_pre])
-    t_c = V(vec.quantize_mx, T.qb0[:, 96:224], T.sb0[:, 96:224], T.h0[:, :], deps=[t_s])
-    t_cs = t_c
-    send2([("c1", "qb0", 96, 128), ("s1", "sb0", 0, 128)], [t_c])
+    def g1():
+        t_g[1] = gauge(1, "q")
+
+    def g2():
+        t_g[2] = gauge(2, "q")
+    together(ids_send(0, "idf"), prep(0), [g1, g2, None, None, lambda: t_ws.append(quant_w(0))])
+
+    m = merge_list(0)
+    t_r = expert(0, 32, [t_ws[0], t_i0, arr("c0"), arr("s0")], m)
+    t_c = V("a", vec.quantize_mx, T.qb0[:, 96:224], T.sb0[:, 96:224], T.h0[:, :], deps=t_r)
+    t_cc = [t_c]
+    send2([("c1", "qb0", 96, 128), ("s1", "sb0", 0, 128)], t_cc)
+    t_mo = m[2]()
+    send("i1", "his", 0, 1, [arr("i0")])
 
     for b in (1, 2):
-        t_m = merge(b - 1, "b%d" % b, [t_c, t_cs, t_mo])
-        if b == 2:
-            t_lg = gather_L(2, [t_mo, t_pre])
+        win = "b%d" % (b - 1)
+        t_m = pick("a", "b%d" % b, 0, win, 128, mo(b - 1), 96, t_cc + [t_mo] + now())
+        t_lg = S("s2", T.lg[:, :], T.iot[:, 0:128].indirect(mo(b - 1)), AF.Copy)
         t_st = score(b, "b%d" % b, t_m + [t_i1])
-        lg = T["lg%d" % b]
-        V(vec.tensor_tensor, T.dl[:, :], lg[:, 1:97], lg[:, 0:96], OP.subtract, deps=[t_lg])
-        t_wn = V(vec.tensor_scalar, T.wn[:, :], T["ps%d" % b][:, 0:96], 0.0, 256.0, OP.is_lt, OP.mult, deps=[t_st])
-        t_nw, t_kk = nonwant(b, t_wn)
-        V(vec.tensor_tensor_scan, T.zc[:, :], T.wn[:, :], T.dl[:, :], 0.0, OP.add, OP.add)
-        V(vec.tensor_tensor, T.xk[:, :], T.zc[:, :], T.nw[:, :], OP.add, deps=[t_nw])
-        t_y0 = V(vec.tensor_scalar, T.y0[:, 0:96], T.xk[:, :], hi[0], lo[0], OP.min, OP.max)
-        V(vec.tensor_scalar, T.y1[:, 0:96], T.xk[:, :], hi[1], lo[1], OP.min, OP.max)
-        t_ac = S(T.jk[:, 0:97], T.y0[:, 0:97], AF.Copy, accum_out=T.acc[:, 0:1], deps=[t_y0])
-        V(vec.tensor_reduce, T.acc[:, 1:2], T.y1[:, 0:97], AxisListType.X, OP.add)
-        t_lo = V(vec.tensor_scalar, T.lo[:, 2 * b:2 * b + 2], T.acc[:, 0:2], 127.0, 0.0, OP.min, OP.max, deps=[t_ac])
+        if b == 2:
+            ids_pick("iw1", 96, 32, "idp", T.ll[:, 2:4], [])
+        ps = T["ps%d" % b]
+        V("a", vec.tensor_scalar, T.wn[:, :], ps[:, 0:96], 0.0, 256.0, OP.is_lt, OP.mult, deps=[t_st])
+        V("b", vec.tensor_scalar, T.nw[:, :], ps[:, 0:96], 0.0, BIG, OP.is_ge, OP.mult)
+        t_zc = V("a", vec.tensor_tensor_scan, T.zc[:, :], T.wn[:, :], T.zz[:, :], 0.0, OP.add, OP.add)
+        t_nl = V("b", vec.tensor_tensor, T.nl[:, :], T.nw[:, :], T.lg[:, :], OP.add, deps=[t_lg])
+        t_kk = V("p", vec.tensor_scalar, T.kk[:, b:b + 1], T.zc[:, 95:96], 256.0 * CAP, None, OP.min, deps=[t_zc])
+        V("a", vec.tensor_tensor, T.xk[:, :], T.zc[:, :], T.nl[:, :], OP.add, deps=[t_nl])
+        t_y0 = V("a", vec.tensor_scalar, T.y0[:, 0:96], T.xk[:, :], hi[0], lo[0], OP.min, OP.max)
+        V("b", vec.tensor_scalar, T.y1[:, 0:96], T.xk[:, :], hi[1], lo[1], OP.min, OP.max)
+        t_a0 = S("s1", T.jk[:, 0:97], T.y0[:, 0:97], AF.Copy, accum_out=T.acc[:, 0:1], deps=[t_y0])
+        t_a1 = V("b", vec.tensor_reduce, T.acc[:, 1:2], T.y1[:, 0:97], AxisListType.X, OP.add)
+        t_lo = V("a", vec.tensor_scalar, T.lo[:, 2 * b:2 * b + 2], T.acc[:, 0:2], 127.0, 0.0, OP.min, OP.max, deps=[t_a0, t_a1])
         send("k%d" % b, "kk", b, b + 1, [t_kk])
         send("l%d" % b, "lo", 2 * b, 2 * b + 2, [t_lo])
         if b == 1:
             send("u2", "qb1", 0, 96, t_m)
             t_w[2] = DMA(g.sync, "y", "lw2", T.wt2[:, :], T.w[:, 4096:6144], [t_lo])
-        t_wq = quant_w(b)
-        V(vec.tensor_tensor, T.cw[:, :], T.xk[:, :], lg[:, 1:97], OP.subtract)
-        merge_prep()
-        ids_take(b - 1, T["iw%d" % b][:, 0:96])
-        ids_send(b, "iw%d" % (b - 1))
-        if b == 1:
-            t_qv = V(vec.quantize_mx, T.qv[:, :], T.sv[:, :], T.vt[:, :], deps=[t_v])
-        count_out(b - 1)
-        early = ["w0", "w1", "u1"] if b == 1 else ["u2"]
-        t_s, _ = expert(b, 128, [t_wq] + [arr(f) for f in early + ["c%d" % b, "s%d" % b]])
-        t_e = V(vec.quantize_mx, T["qe%d" % b][:, :], T["se%d" % b][:, :], T["h%d" % b][:, :], deps=[t_s])
-        t_mo = merge_list(b)
-        off = T.ll[:, 2 * b:2 * b + 2]
-        d = [t_e, t_i1, arr("l%d" % b)]
-        t_cs = S(T["sb%d" % b][:, 96:128], T["se%d" % b][:, 0:128].indirect(off), AF.Copy, deps=d)
-        t_c = V(vec.tensor_copy, codes(T["qb%d" % b][:, 96:128]), codes(T["qe%d" % b][:, 0:128]).indirect(off), deps=d)
-        if b == 1:
-            send2([("c2", "qb1", 96, 128), ("s2", "sb1", 0, 128)], [t_c, t_cs])
+        t_ws = []
 
-    t_m = merge(2, "f", [t_c, t_cs, t_mo])
-    t_st = MM("st", T.pv[:, 0:128], (T.qv[:, 0:128], T.sv[:, 0:128]), (T.qf[:, 0:128], T.sf[:, 0:128]), [t_qv, t_i1] + t_m)
-    DMA(g.sync, "y", "oc1", T.oc[:, 0:4 * PL], T.qf[:, 0:96].bitcast(dt.uint8), [t_m[1]])
+        def qv():
+            t_ws.append(V("q", vec.quantize_mx, T.qv[:, :], T.sv[:, :], T.vt[:, :], deps=[t_v]))
+        if b == 1:
+            together(prep(1), [lambda: t_ws.append(quant_w(1)), qv], ids_take(0, "iw0"))
+            t_qv = t_ws[1]
+            ids_pick("iw1", 0, 96, "iw0", mo(0), [t_mo])
+        else:
+            together(ids_send(2, "iw1"), prep(2), [None, None, None, lambda: t_ws.append(quant_w(2))])
+            ids_pick("iw2", 0, 96, "iw1", mo(1), [t_mo])
+        V("q", vec.tensor_scalar, T.ksb[:, b - 1:b], T.kk[:, b - 1:b], T.ko[:, b - 1:b], 1.0 / 256, OP.min, OP.mult)
+        t_r = expert(b, 128, [t_ws[0]] + t_r + [arr(f) for f in (("w0", "w1") if b == 1 else ()) + ("u%d" % b, "c%d" % b, "s%d" % b)], None)
+        t_e = V("a", vec.quantize_mx, T["qe%d" % b][:, :], T["se%d" % b][:, :], T["h%d" % b][:, :], deps=t_r)
+        m = merge_list(b)
+        if b == 1:
+            together(ids_take(1, "idp"), m[:2])
+        else:
+            m[0]()
+            m[1]()
+        t_mo = m[2]()
+        t_cc = pick("a", "b%d" % b, 96, "e%d" % b, 128, T.ll[:, 2 * b:2 * b + 2], 32, [t_e, t_i1, arr("l%d" % b)])
+        if b == 1:
+            send2([("c2", "qb1", 96, 128), ("s2", "sb1", 0, 128)], t_cc)
+
+    t_m = pick("a", "f", 0, "b2", 128, mo(2), 96, t_cc + [t_mo])
+    t_st = MM("st", T.pv, ("v", 0), ("f", 0), [t_qv, t_i1] + t_m)
+    DMA(g.sync, "y", "oc1", T.oc[:, 0:4 * PL], T.qf[:, 0:96].bitcast(dt.uint8), t_m[:1])
     for k in range(4):
-        DMA(g.scalar, "s", "oc2", T.osc[4 * k:4 * k + 4, 0:PL], T.sf[32 * k:32 * k + 4, 0:96], [t_m[0]])
-    t_y = V(vec.tensor_copy, T.yb[:, :], T.pv[:, 0:96], deps=[t_st])
+        DMA(g.scalar, "s", "oc2", T.osc[4 * k:4 * k + 4, 0:PL], T.sf[32 * k:32 * k + 4, 0:96], t_m[1:])
+    t_ks = V("q", vec.tensor_scalar, T.ksb[:, 2:3], T.kk[:, 2:3], T.ko[:, 2:3], 1.0 / 256, OP.min, OP.mult)
+    t_y = V("a", vec.tensor_copy, T.yb[:, :], T.pv[:, 0:96], deps=[t_st])
     DMA(g.sync, "y", "oy", T.y[:, :], T.yb[:, :], [t_y])
-    t_id = ids_take(2, T.idl[:, :])
-    DMA(g.scalar, "s", "oi", T.ids[0:1, :], T.idl[0:1, :], [t_id])
-    count_out(2)
-    t_ks = V(vec.tensor_scalar, T.ksb[:, :], T.ksr[:, :], 1.0 / 256, None, OP.mult)
     DMA(g.sync, "y", "oi", T.ks[0:1, :], T.ksb[0:1, :], [t_ks])
+    together(ids_take(2, "iw2"))
+    t_id = ids_pick("idl", 0, 96, "iw2", mo(2), [t_mo])
+    DMA(g.scalar, "s", "oi", T.ids[0:1, :], T.idl[0:1, :], [t_id])
     need("g", g, [(s, n) for s, n in cnt.items() if n] + [arr(f) for f in FLOWS])

@@ -1,5 +1,5 @@
 from concourse.bass import DstId, RemoteDMATransfer
-from concourse.mybir import dt, AluOpType, AxisListType, ActivationFunctionType
+from concourse.mybir import dt, AluOpType, ActivationFunctionType
 
 PL, L, CAP = 96, 3, 32
 OP, AF = AluOpType, ActivationFunctionType
@@ -18,17 +18,19 @@ def _pair(name, n):
     _buf("s" + name, n, U8)
 
 
-for _n, _w in (("xt", 512), ("ut", 512), ("vt", 512), ("wt0", 2048), ("wt1", 2048), ("wt2", 2048), ("h0", 512), ("h1", 512), ("h2", 512)):
+for _n, _w in (("xt", 512), ("ut", 512), ("vt", 512), ("zt", 512), ("wt0", 2048), ("wt1", 2048), ("wt2", 2048), ("h0", 512), ("h1", 512), ("h2", 512),
+               ("zc", 96 * L)):
     _buf(_n, _w, BF)
-for _n, _w in (("a", 128), ("u", 128), ("g0", 128), ("g1", 128), ("g2", 128), ("w0", 512), ("w1", 512), ("w2", 512), ("v", 128),
-               ("b0", 224), ("b1", 128), ("b2", 128), ("f", 128), ("o0", 32), ("d0", 128), ("d1", 128), ("d2", 128), ("e1", 128), ("e2", 128)):
+for _n, _w in (("u", 128), ("g0", 128), ("g1", 128), ("g2", 128), ("w0", 512), ("w1", 512), ("w2", 512), ("v", 128),
+               ("b0", 128), ("b1", 224), ("b2", 224), ("f", 96), ("d0", 224), ("d1", 224), ("d2", 224), ("e0", 128), ("e1", 128), ("e2", 128)):
     _pair(_n, _w)
-for _n in ("ps0", "ps1", "ps2", "pr0", "pr1", "pr2", "pr3", "pv"):
+for _n in ("psa", "pse", "pr0", "pr1", "pr2", "pr3"):
     _buf(_n, 512, F32, "psum")
-for _n, _w in (("iot", 128), ("idf", 128), ("idp", 128), ("t16", 96), ("p6", 6), ("cc", 8), ("mk", 96), ("rs", 96), ("zz", 96), ("dd0", 12), ("dd1", 12),
-               ("so", 12), ("wn", 96), ("nw", 96), ("nl", 96), ("zc", 96), ("xk", 96), ("jk", 97), ("jk2", 96), ("y0", 97), ("y1", 97), ("acc", 4), ("cw", 96),
-               ("dg", 96), ("ds", 96), ("t6", 6), ("lg", 96), ("si", 32), ("sit", 32), ("rc", 1), ("rb", 32),
-               ("iw0", 128), ("iw1", 128), ("iw2", 128), ("idl", 96), ("ksb", 3), ("yb", 96)):
+for _n, _w in (("t16", 96), ("p18", 18), ("cc", 4), ("mk", 96), ("rs", 96), ("zz", 96), ("dd0", 12 * L), ("dd1", 12 * L), ("so", 12 * L),
+               ("wn", 96 * L), ("nw", 96 * L), ("jk", 96 * L), ("jk2", 96 * L), ("acc", 2 * L), ("cw", 96 * L), ("dg", 96 * L),
+               ("ds", 96 * L), ("t6", 6 * L), ("ov", 6 * L), ("dx", 6 * L), ("fe0", 128), ("fe1", 128), ("fe2", 128), ("fw0", 128), ("fw1", 128), ("fw2", 128),
+               ("idp", 128), ("iw0", 128), ("iw1", 128), ("iw2", 128), ("idl", 96), ("si1", 32), ("si2", 32), ("sit1", 32), ("sit2", 32),
+               ("rb1", 32), ("rb2", 32), ("km", 3), ("ksb", 3), ("yb", 96)):
     _buf(_n, _w, F32)
 _buf("iq", 2, I32)
 _buf("iqa", 2, I32)
@@ -36,31 +38,31 @@ _buf("cf", 8 * L, U16)
 _buf("mo", 8 * L, U16)
 _buf("lo", 2 * L, U16)
 _buf("ll", 2 * L, U16)
-_buf("kk", L, BF)
 _buf("ko", L, BF)
 _buf("mine", L, U16)
 _buf("his", L, U16)
-for _n, _w in (("xw0", 16), ("xw1", 16), ("xu1", 64), ("xu2", 96), ("xc0", 32), ("xc1", 32), ("xc2", 32)):
-    _buf(_n, _w, F8)
-for _n, _w in (("xs0", 32), ("xs1", 128), ("xs2", 128)):
-    _buf(_n, _w, U8)
+for _b in range(L):
+    _buf("xa%d" % _b, 48, F8)
+    _buf("xb%d" % _b, 48, F8)
+    _buf("xs%d" % _b, 96, U8)
 _buf("xks", L, BF)
 _buf("xis", L, U16)
 _buf("xls", 2 * L, U16)
 
-FLOWS = {
-    "w0": (0, 1, "xw0", 0, "qd1", 0, 16), "w1": (1, 1, "xw1", 0, "qd1", 16, 16), "u1": (2, 1, "xu1", 0, "qd1", 32, 64), "u2": (2, 2, "xu2", 0, "qd2", 0, 96),
-    "c0": (0, 0, "xc0", 0, "qd0", 0, 32), "c1": (0, 1, "xc1", 0, "qd1", 96, 32), "c2": (0, 2, "xc2", 0, "qd2", 96, 32),
-    "s0": (1, 0, "xs0", 0, "sd0", 0, 32), "s1": (1, 1, "xs1", 0, "sd1", 0, 128), "s2": (1, 2, "xs2", 0, "sd2", 0, 128),
-    "k0": (1, 0, "xks", 0, "ko", 0, 1), "k1": (1, 1, "xks", 1, "ko", 1, 1), "k2": (1, 2, "xks", 2, "ko", 2, 1),
-    "l1": (0, 1, "xls", 2, "ll", 2, 2), "l2": (0, 2, "xls", 4, "ll", 4, 2),
-    "i0": (2, 0, "xis", 0, "his", 0, 1), "i1": (2, 1, "xis", 1, "his", 1, 1), "i2": (2, 2, "xis", 2, "his", 2, 1),
-}
-ORDER = (("w0", "c0", "c1", "l1", "c2", "l2"), ("w1", "s0", "k0", "s1", "k1", "s2", "k2"), ("u1", "i0", "i1", "u2", "i2"))
+FLOWS = {}
+for _b in range(L):
+    FLOWS["a%d" % _b] = (0, _b, "xa%d" % _b, 0, "qd%d" % _b, 0, 48)
+    FLOWS["b%d" % _b] = (2, _b, "xb%d" % _b, 0, "qd%d" % _b, 48, 48)
+    FLOWS["s%d" % _b] = (1, _b, "xs%d" % _b, 0, "sd%d" % _b, 0, 96)
+    FLOWS["k%d" % _b] = (0, _b, "xks", _b, "ko", _b, 1)
+    FLOWS["l%d" % _b] = (0, _b, "xls", 2 * _b, "ll", 2 * _b, 2)
+    if _b:
+        FLOWS["i%d" % _b] = (1, _b, "xis", _b, "his", _b, 1)
+ORDER = (("a0", "k0", "l0", "a1", "k1", "l1", "a2", "k2", "l2"), ("s0", "s1", "i1", "s2", "i2"), ("b0", "b1", "b2"))
 
-VCH, SCH = ["va", "vb", "vp", "vi", "vq", "vk", "vm", "vc"], ["s1", "s2"]
-SEMAPHORES = (["a_" + f for f in FLOWS] + VCH + SCH + ["st", "r0", "r1", "r2", "r3", "sg", "sq", "lsa", "lsb", "lx", "lu", "lw0", "lw1", "lw2", "lv",
-              "li0", "li1", "oy", "oc1", "oc2", "oi"])
+VCH, SCH = ["va", "vc", "ve", "vf", "vp", "vi", "vq", "vk", "vm", "vt"], ["s1", "s2", "s3", "s4"]
+SEMAPHORES = (["a_" + f for f in FLOWS] + VCH + SCH + ["st", "r0", "r1", "r2", "r3", "sq", "sg", "sh", "lsa", "ls0", "ls1", "ls2", "lx", "lu", "lv",
+              "oy", "oc1", "oc2", "oi", "ok"] + ["lw%d%d" % (_b, _i) for _b in range(L) for _i in range(4)])
 
 
 def _raw(view, name):
@@ -82,11 +84,7 @@ def _relays(core, T, topo):
 def _hop1(f, src, dst, topo):
     es = topo.engines(src, dst)
     h = len(es) // 2
-    if f in ("w0", "c1", "c2"):
-        return es[:h]
-    if f in ("w1", "s1", "s2"):
-        return es[h:]
-    return es
+    return es[:h] if f[0] == "a" else es[h:] if f[0] == "b" else es
 
 
 def _relay_program(g, core, me, partners, T, topo, rankcore):
@@ -112,15 +110,18 @@ def rank_program(g, core, T, topo):
                     _relay_program(g, core, rel.index(core), partners, T, topo, rc)
         return
     rel, partners = _relays(core, T, topo)
-    cnt = {"lsa": 0, "lsb": 0}
+    cnt = {}
     seen = {}
     vec = g.vector
 
     def need(q, eng, toks):
+        best = {}
         for s, n in toks:
             if seen.get((q, s), 0) < n:
-                eng.wait_ge(T.sem[s], n)
-                seen[(q, s)] = n
+                best[s] = max(n, best.get(s, 0))
+        for s in best:
+            eng.wait_ge(T.sem[s], best[s])
+            seen[(q, s)] = best[s]
 
     def bump(s, ins, n=1):
         ins.then_inc(T.sem[s], n)
@@ -149,235 +150,269 @@ def rank_program(g, core, T, topo):
         need(q, eng, deps)
         return bump(s, eng.dma_start(out, in_), 16)
 
-    def pick(ch, out, a, win, n, off, w, deps=()):
-        s = S("s1", T["s" + out][:, a:a + w], T["s" + win][:, 0:n].indirect(off), AF.Copy, deps=deps)
-        v = V(ch, vec.tensor_copy, T["q" + out][:, a:a + w].bitcast(dt.uint32), T["q" + win][:, 0:n].bitcast(dt.uint32).indirect(off), deps=deps)
-        return [v, s]
+    def pick_s(out, a, win, off, w, deps=()):
+        return S("s1", T["s" + out][:, a:a + w], T["s" + win][:, 0:128].indirect(off), AF.Copy, deps=deps)
+
+    def pick_v(ch, out, a, win, off, w, deps=()):
+        return V(ch, vec.tensor_copy, T["q" + out][:, a:a + w].bitcast(dt.uint32), T["q" + win][:, 0:128].bitcast(dt.uint32).indirect(off), deps=deps)
 
     def hop1(f, name, a, b):
         k, _, xb, xa, _, _, w = FLOWS[f]
         rid, pid = topo.addr(rel[k], core)
         return rid, pid, _hop1(f, core, rel[k], topo), _raw(T[xb][:, xa:xa + w], xb), _raw(T[name][:, a:b], name)
 
-    def send(f, name, a, b, deps, ls="lsb"):
+    def left(b):
+        return ("ls%d" % b, cnt["ls%d" % b])
+
+    def send(f, name, a, b, deps):
         need("g", g, deps)
         rid, pid, es, out, in_ = hop1(f, name, a, b)
+        ls = "ls%d" % FLOWS[f][1]
         g.remote_dma(out, in_, T.sem["a_" + f], T.sem[ls], pid, rid, _mask(es))
-        cnt[ls] += len(es)
+        cnt[ls] = cnt.get(ls, 0) + len(es)
 
-    def send2(parts, deps, ls="lsb"):
+    def send2(parts, deps):
         need("g", g, deps)
         tr = []
         for f, name, a, b in parts:
             rid, pid, es, out, in_ = hop1(f, name, a, b)
+            ls = "ls%d" % FLOWS[f][1]
             tr.append(RemoteDMATransfer(dst_ids=[DstId(rid=rid, pnc=pid)], dma_engine_mask=_mask(es), remote_sem=T.sem["a_" + f], srcs=[in_], dsts=[out]))
-            cnt[ls] += len(es)
+            cnt[ls] = cnt.get(ls, 0) + len(es)
         g.remote_dma_fused(tr, local_sem=T.sem[ls])
 
     def arr(f):
         src = _relays(partners[FLOWS[f][1]], T, topo)[0][FLOWS[f][0]]
         return ("a_" + f, len(topo.engines(src, core)))
 
-    def together(*chains):
-        for k in range(max(len(c) for c in chains)):
-            for c in chains:
-                if k < len(c) and c[k]:
-                    c[k]()
+    def columns(b, tq, ts):
+        send2([("a%d" % b, "qb%d" % b, 0, 48), ("b%d" % b, "qb%d" % b, 48, 96)], [tq])
+        send("s%d" % b, "sb%d" % b, 0, 96, [ts])
 
-    t_u = DMA(g.sync, "y", "lu", T.ut[:, 0:16], T.u[:, 0:16])
-    t_x = DMA(g.scalar, "s", "lx", T.xt[:, 0:4 * PL], T.x[:, 0:4 * PL])
-    t_w = [DMA(g.sync, "y", "lw0", T.wt0[:, :], T.w[:, 0:2048]), None, None]
-
-    def iota(buf, n, pattern, base, cm):
-        return bump("sg", g.iota(T[buf][:, 0:n], pattern, base, cm, allow_small_or_imprecise_dtypes=True))
-    t_iq = bump("sq", g.iota(T.iq[:, 0:2], [[0, 2]], 0, 1))
-    iota("t16", 96, [[0, 6], [1, 16]], 0, 0)
-    iota("p6", 6, [[16, 6]], 0, 0)
-    iota("iot", 128, [[1, 128]], 0, 0)
-    iota("idf", 128, [[1, 128]], rank * PL, 0)
-    iota("idp", 128, [[1, 128]], T.rank_of(partners[1]) * PL, 0)
-    t_io = iota("iw0", 96, [[1, 96]], rank * PL, 0)
-
-    V("k", vec.memset, T.ut[:, 16:512], 0.0, free=True)
-    V("k", vec.memset, T.xt[:, 384:512], 0.0, free=True)
-    for b in range(L):
-        V("k", vec.memset, T.cf[:, 8 * b:8 * b + 8], b, free=True)
-    V("k", vec.memset, T.dd0[:, :], 0.0, free=True)
-    V("k", vec.memset, T.h0[:, 128:512], 0.0, free=True)
-    V("k", vec.memset, T.zz[:, :], 0.0, free=True)
-    t_k = now("vk")
-    ic, jb0, jb1 = T.cc[:, 0:1], T.cc[:, 1:2], T.cc[:, 2:3]
-    lo, hi = (T.cc[:, 3:4], T.cc[:, 4:5]), (T.cc[:, 5:6], T.cc[:, 6:7])
-    V("c", vec.tensor_scalar, T.iqa[:, :], T.iq[:, :], 15, None, OP.bitwise_and, deps=[t_iq])
-    V("c", vec.tensor_copy, ic, T.iqa[:, 0:1])
-    V("c", vec.tensor_scalar, jb0, ic, 256.0, 128.0, OP.mult, OP.add)
-    t_jc = V("c", vec.tensor_scalar, jb1, ic, 256.0, 4224.0, OP.mult, OP.add)
-    t_qu = V("a", vec.quantize_mx, T.qu[:, :], T.su[:, :], T.ut[:, :], deps=[t_u] + t_k)
-
-    def gauge(b, ch):
-        return pick(ch, "g%d" % b, 0, "u", 128, T.cf[:, 8 * b:8 * b + 8], 128, [t_qu] + t_k)
-    t_g = [gauge(0, "a"), None, None]
-    t_qb = V("b", vec.quantize_mx, T.qb0[:, 0:128], T.sb0[:, 0:128], T.xt[:, :], deps=[t_x])
-    send("u1", "qb0", 32, 96, [t_qb])
-    send2([("w0", "qb0", 0, 16), ("w1", "qb0", 16, 32)], [t_qb])
-
-    def score(b, q, deps):
-        return MM("st", T["ps%d" % b], ("g%d" % b, 0), (q, 0), t_g[b] + deps)
-
-    t_st = score(0, "b0", [t_qb])
-    t_qa = V("q", vec.quantize_mx, T.qa[:, :], T.sa[:, :], T.xt[:, :])
-    V("a", vec.tensor_scalar, T.wn[:, :], T.ps0[:, 0:96], 0.0, 256.0, OP.is_lt, OP.mult, deps=[t_st])
-    V("b", vec.tensor_scalar, T.nw[:, :], T.ps0[:, 0:96], 0.0, BIG, OP.is_ge, OP.mult)
-    t_zc = V("a", vec.tensor_tensor_scan, T.zc[:, :], T.wn[:, :], T.zz[:, :], 0.0, OP.add, OP.add)
-    t_a0 = S("s1", T.jk[:, 0:96], T.zc[:, :], AF.Sign, bias=jb0, scale=-1.0, accum_out=T.acc[:, 0:1], deps=[t_zc, t_jc])
-    t_a1 = S("s2", T.jk2[:, 0:96], T.zc[:, :], AF.Sign, bias=jb1, scale=-1.0, accum_out=T.acc[:, 1:2])
-    t_k0 = V("b", vec.tensor_scalar, T.kk[:, 0:1], T.zc[:, 95:96], 256.0 * CAP, None, OP.min, deps=[t_zc])
-    t_lo = V("a", vec.tensor_scalar, T.lo[:, 0:2], T.acc[:, 0:2], 96.0, 0.5, OP.add, OP.mult, deps=[t_a0, t_a1])
-    t_o = pick("a", "o0", 0, "a", 128, T.lo[:, 0:2], 32, [t_lo, t_qa])
-    send("c0", "qo0", 0, 32, t_o[:1], "lsa")
-    send("s0", "so0", 0, 32, t_o[1:], "lsa")
-    send("k0", "kk", 0, 1, [t_k0], "lsa")
-    DMA(g.sync, "y", "li0", T.qd0[:, 32:128].bitcast(dt.uint8), T.qa[:, 0:96].bitcast(dt.uint8), [t_qa, ("lsa", cnt["lsa"])])
-    t_i0 = DMA(g.sync, "y", "li0", T.sd0[:, 32:128], T.sa[:, 0:96])
-    for q in ("b1", "b2", "f"):
-        DMA(g.sync, "y", "li1", T["q" + q][:, 96:128].bitcast(dt.uint8), T.qa[:, 96:128].bitcast(dt.uint8))
-        t_i1 = DMA(g.sync, "y", "li1", T["s" + q][:, 96:128], T.sa[:, 96:128])
-    t_w[1] = DMA(g.sync, "y", "lw1", T.wt1[:, :], T.w[:, 2048:4096])
-    t_v = DMA(g.sync, "y", "lv", T.vt[:, :], T.v[:, :])
-
-    def prep(b):
-        def t6():
-            S("s2", T.t6[:, :], T.ds[:, 15:96:16], AF.Identity, bias=PL - 1.0, scale=1.0 / 256, deps=now("vp"))
-        return [lambda: V("p", vec.tensor_tensor, T.cw[:, :], T.zc[:, :], T.nw[:, :], OP.add, deps=now("va", "vb")),
-                lambda: V("p", vec.tensor_tensor, T.dg[:, :], T.cw[:, :], T.mk[:, :], OP.mult),
-                lambda: V("p", vec.tensor_tensor_scan, T.ds[:, :], T.rs[:, :], T.dg[:, :], 0.0, OP.mult, OP.add),
-                t6,
-                lambda: V("p", vec.tensor_tensor, T.dd1[:, 0:12:2], T.t6[:, :], T.dd1[:, 1:12:2], OP.subtract, deps=now("s2"))]
-
-    def merge_list(b):
-        return [lambda: V("m", vec.tensor_scalar, T.dd0[:, 1:12:2], T.ds[:, 15:96:16], T.ko[:, b:b + 1], None, OP.is_le, deps=[arr("k%d" % b)] + now("vp")),
-                lambda: V("m", vec.tensor_tensor_scan, T.so[:, :], T.dd0[:, :], T.dd1[:, :], 0.0, OP.mult, OP.add),
-                lambda: V("m", vec.tensor_copy, T.mo[:, 8 * b:8 * b + 6], T.so[:, 1:12:2])]
+    def c(name, b, w=PL):
+        return T[name][:, w * b:w * b + w]
 
     def mo(b):
         return T.mo[:, 8 * b:8 * b + 6]
 
-    def ids_send(b, win):
+    def ll(b):
+        return T.ll[:, 2 * b:2 * b + 2]
+
+    t_u = DMA(g.sync, "y", "lu", T.ut[:, 0:16], T.u[:, 0:16])
+    t_x = DMA(g.scalar, "s", "lx", T.xt[:, 0:4 * PL], T.x[:, 0:4 * PL])
+
+    def load_w(b, deps=()):
+        return [DMA(g.sync, "y", "lw%d%d" % (b, i), T["wt%d" % b][:, 512 * i:512 * i + 512], T.w[:, 2048 * b + 512 * i:2048 * b + 512 * i + 512], deps)
+                for i in range(4)]
+    t_lw = [load_w(0), None, None]
+
+    def iota(s, view, pattern, base, cm):
+        return bump(s, g.iota(view, pattern, base, cm, allow_small_or_imprecise_dtypes=True))
+    t_iq = bump("sq", g.iota(T.iq[:, 0:2], [[0, 2]], 0, 1))
+    iota("sg", T.t16[:, 0:96], [[0, 6], [1, 16]], 0, 0)
+    t_io = iota("sg", T.p18[:, 0:18], [[0, 3], [16, 6]], 0, 0)
+
+    V("k", vec.memset, T.ut[:, 16:512], 0.0, free=True)
+    V("k", vec.memset, T.cf[:, 0:8], 0, free=True)
+    V("k", vec.memset, T.xt[:, 384:512], 0.0, free=True)
+    V("k", vec.memset, T.zz[:, :], 0.0, free=True)
+    t_k = now("vk")
+    ic, jb0, jb1 = T.cc[:, 0:1], T.cc[:, 1:2], T.cc[:, 2:3]
+    V("c", vec.tensor_scalar, T.iqa[:, :], T.iq[:, :], 15, None, OP.bitwise_and, deps=[t_iq])
+    V("k", vec.memset, T.zt[:, :], 0.0, free=True)
+    t_ic = V("c", vec.tensor_copy, ic, T.iqa[:, 0:1])
+    V("k", vec.memset, T.cf[:, 8:16], 1, free=True)
+    V("k", vec.memset, T.cf[:, 16:24], 2, free=True)
+    V("t", vec.tensor_scalar, jb0, ic, 256.0, 128.0, OP.mult, OP.add, deps=[t_ic])
+    t_jc = V("t", vec.tensor_scalar, jb1, ic, 256.0, 4224.0, OP.mult, OP.add, free=True)
+    V("k", vec.memset, T.dd0[:, :], 0.0, free=True)
+    V("k", vec.memset, T.h0[:, 384:512], 0.0, free=True)
+    t_qu = V("a", vec.quantize_mx, T.qu[:, :], T.su[:, :], T.ut[:, :], deps=[t_u] + t_k)
+    t_qb = V("q", vec.quantize_mx, T.qb0[:, :], T.sb0[:, :], T.xt[:, :], deps=[t_x])
+
+    def gauge(b, ch):
+        off = T.cf[:, 8 * b:8 * b + 8]
+        s = pick_s("g%d" % b, 0, "u", off, 128, [t_qu] + now("vk"))
+        return [pick_v(ch, "g%d" % b, 0, "u", off, 128, [t_qu] + now("vk")), s]
+    t_g = [gauge(0, "a"), None, None]
+    columns(0, t_qb, t_qb)
+    t_mm = MM("st", T.psa, ("g0", 0), ("b0", 0), t_g[0] + [t_qb])
+
+    def zeros(*names):
+        for n in names:
+            V("q", vec.quantize_mx, T["q" + n][:, 96:224], T["s" + n][:, 96:224], T.zt[:, :], deps=now("vk"), free=True)
+
+    def make_list(b, t_wn, gap1, gap2):
+        t_zc = V("a", vec.tensor_tensor_scan, c("zc", b), c("wn", b), T.zz[:, :], 0.0, OP.add, OP.add)
+        a0 = S("s2", c("jk", b), c("zc", b), AF.Sign, bias=jb0, scale=-1.0, accum_out=T.acc[:, 2 * b:2 * b + 1], deps=[t_zc, t_jc])
+        a1 = S("s3", c("jk2", b), c("zc", b), AF.Sign, bias=jb1, scale=-1.0, accum_out=T.acc[:, 2 * b + 1:2 * b + 2])
+        t_nw = S("s4", c("nw", b), c("wn", b), AF.Identity, bias=BIG, scale=-BIG / 256, deps=[t_wn])
+        send("k%d" % b, "zc", 96 * b + 95, 96 * b + 96, [t_zc])
+        gap1()
+        t_lo = V("a", vec.tensor_scalar, T.lo[:, 2 * b:2 * b + 2], T.acc[:, 2 * b:2 * b + 2], 96.0, 0.5, OP.add, OP.mult, deps=[a0, a1])
+        send("l%d" % b, "lo", 2 * b, 2 * b + 2, [t_lo])
+        gap2(t_lo)
+        return t_zc, t_nw
+
+    def prep(b, t_zc, t_nw):
+        ds, d1 = T.ds[:, 96 * b + 15:96 * b + 96:16], T.dd1[:, 12 * b:12 * b + 12:2]
+        t = []
+
+        def small():
+            d = now("vp")
+            t.append(S("s4", c("t6", b, 6), ds, AF.Identity, bias=PL - 1.0, scale=1.0 / 256, deps=d))
+            t.append(S("s2", c("ov", b, 6), ds, AF.Relu, scale=64.0, bias=T.cc[:, 3:4], deps=d + now("vt")))
+
         def last():
-            t = V("i", vec.tensor_copy, T.mine[:, b:b + 1], T.sit[:, 0:1])
-            send("i%d" % b, "mine", b, b + 1, [t])
-        return [lambda: V("i", vec.tensor_copy, T.si[:, 0:32], T[win][:, 0:128].indirect(T.lo[:, 2 * b:2 * b + 2]), deps=now("va")),
-                lambda: V("i", vec.transpose, T.sit[:, :], T.si[:, :]), last]
+            V("p", vec.tensor_tensor, d1, c("t6", b, 6), T.dd1[:, 12 * b + 1:12 * b + 12:2], OP.subtract, deps=t[:1])
+            V("p", vec.tensor_tensor, c("dx", b, 6), c("ov", b, 6), ds, OP.add, deps=t[1:], free=True)
+        return [lambda: V("p", vec.tensor_tensor, c("cw", b), c("zc", b), c("nw", b), OP.add, deps=[t_zc, t_nw]),
+                lambda: V("p", vec.tensor_tensor, c("dg", b), c("cw", b), T.mk[:, :], OP.mult, deps=now("vt")),
+                lambda: V("p", vec.tensor_tensor_scan, c("ds", b), T.rs[:, :], c("dg", b), 0.0, OP.mult, OP.add),
+                small, last]
 
-    def ids_take(b, out):
-        return [lambda: V("i", vec.tensor_copy, T.rc[:, :], T.his[:, b:b + 1], deps=[arr("i%d" % b)]),
-                lambda: V("i", vec.tensor_scalar, T.rb[:, :], T.zz[:, 0:32], T.rc[:, 0:1], None, OP.add),
-                lambda: V("i", vec.transpose, T[out][:, 96:128], T.rb[:, :])]
+    def merge_list(b):
+        return [lambda: V("m", vec.tensor_scalar, T.dd0[:, 12 * b + 1:12 * b + 12:2], c("dx", b, 6), T.ko[:, b:b + 1], None, OP.is_le,
+                          deps=[arr("k%d" % b)] + now("vp", "vk")),
+                lambda: V("m", vec.tensor_tensor_scan, c("so", b, 12), c("dd0", b, 12), c("dd1", b, 12), 0.0, OP.mult, OP.add),
+                lambda: V("m", vec.tensor_copy, T.mo[:, 8 * b:8 * b + 6], T.so[:, 12 * b + 1:12 * b + 12:2])]
 
-    def ids_pick(out, a, w, win, off, deps):
-        return V("i", vec.tensor_copy, T[out][:, a:a + w], T[win][:, 0:128].indirect(off), deps=deps)
+    def quant_w(b, i):
+        return V("q", vec.quantize_mx, T["qw%d" % b][:, 128 * i:128 * i + 128], T["sw%d" % b][:, 128 * i:128 * i + 128],
+                 T["wt%d" % b][:, 512 * i:512 * i + 512], deps=[t_lw[b][i]], free=True)
 
-    def quant_w(b):
-        return V("q", vec.quantize_mx, T["qw%d" % b][:, :], T["sw%d" % b][:, :], T["wt%d" % b][:, :], deps=[t_w[b]])
-
-    def expert(b, n, deps, between):
-        h = T["h%d" % b]
-        tr = [MM("r%d" % i, T["pr%d" % i], ("w%d" % b, 128 * i), ("d%d" % b, 0), deps) for i in range(4)]
+    def expert(b, tw, deps, m):
+        h, n = T["h%d" % b], PL
+        tr = [MM("r%d" % i, T["pr%d" % i], ("w%d" % b, 128 * i), ("d%d" % b, 0), deps + [tw[i]]) for i in range(4)]
         t0 = S("s1", h[:, 0:4 * n:4], T.pr0[:, 0:n], AF.Copy, scale=0.0625, deps=[tr[0]])
         t2 = S("s2", h[:, 2:4 * n:4], T.pr2[:, 0:n], AF.Copy, scale=0.0625, deps=[tr[2]])
-        t1 = V("a", vec.tensor_scalar, h[:, 1:4 * n:4], T.pr1[:, 0:n], 0.0625, None, OP.mult, deps=[tr[1]])
-        if between:
-            between[0]()
-        t3 = V("b", vec.tensor_scalar, h[:, 3:4 * n:4], T.pr3[:, 0:n], 0.0625, None, OP.mult, deps=[tr[3]])
-        if between:
-            between[1]()
-        return [t0, t1, t2, t3]
+        t1 = V("e", vec.tensor_scalar, h[:, 1:4 * n:4], T.pr1[:, 0:n], 0.0625, None, OP.mult, deps=[tr[1]], free=True)
+        t3 = V("e", vec.tensor_scalar, h[:, 3:4 * n:4], T.pr3[:, 0:n], 0.0625, None, OP.mult, deps=[tr[3]], free=True)
+        t_r = [t0, t1, t2, t3]
+        t_e = V("e", vec.quantize_mx, T["qe%d" % b][:, :], T["se%d" % b][:, :], T["h%d" % b][:, :], deps=t_r + [t_io2] + now("vk"))
+        m[0]()
+        m[1]()
+        return t_r, t_e
 
-    need("v", vec, [t_io])
-    V("c", vec.tensor_scalar, T.mk[:, :], T.t16[:, :], ic, None, OP.is_equal, free=True)
-    V("c", vec.tensor_scalar, T.rs[:, :], T.t16[:, :], 0.0, None, OP.is_gt, free=True)
-    V("c", vec.tensor_scalar, T.dd1[:, 1:12:2], T.p6[:, :], ic, None, OP.add, free=True)
-    for j in (0, 1):
-        V("c", vec.tensor_scalar, lo[j], ic, 256.0, 256.0 + 4096.0 * j, OP.mult, OP.add, free=True)
-        V("c", vec.tensor_scalar, hi[j], ic, 256.0, 511.0 + 4096.0 * j, OP.mult, OP.add, free=True)
-        V("c", vec.tensor_scalar, T["y%d" % j][:, 96:97], ic, -24321.0, -48801.0 - 389136.0 * j, OP.mult, OP.add, free=True)
-    need("v", vec, now("vc"))
-    t_ws = []
+    def flags(buf, n, ps, deps):
+        return V("f", vec.tensor_scalar, T[buf][:, 0:n], ps[:, 0:n], 0.0, 256.0, OP.is_lt, OP.mult, deps=deps, free=True)
 
-    def g1():
-        t_g[1] = gauge(1, "q")
+    def row_numbers(b, deps):
+        return S("s3", T["iw%d" % (b + 1)][:, 0:96], T["iw%d" % b][:, :].indirect(mo(b)), AF.Copy, deps=deps)
 
-    def g2():
-        t_g[2] = gauge(2, "q")
-    together(ids_send(0, "idf"), prep(0), [g1, g2, None, None, lambda: t_ws.append(quant_w(0))])
+    def give_numbers(b, t_lo):
+        t = S("s3", T["si%d" % b][:, :], T["iw%d" % b][:, :].indirect(T.lo[:, 2 * b:2 * b + 2]), AF.Copy, deps=[t_lo])
 
-    m = merge_list(0)
-    t_r = expert(0, 32, [t_ws[0], t_i0, arr("c0"), arr("s0")], m)
-    t_c = V("a", vec.quantize_mx, T.qb0[:, 96:224], T.sb0[:, 96:224], T.h0[:, :], deps=t_r)
-    t_cc = [t_c]
-    send2([("c1", "qb0", 96, 128), ("s1", "sb0", 0, 128)], t_cc)
-    t_mo = m[2]()
-    send("i1", "his", 0, 1, [arr("i0")])
+        def out():
+            send("i%d" % b, "mine", b, b + 1, [V("i", vec.tensor_copy, T.mine[:, b:b + 1], T["sit%d" % b][:, 0:1])])
+        return [lambda: V("i", vec.transpose, T["sit%d" % b][:, :], T["si%d" % b][:, :], deps=[t]), out]
 
+    def take_numbers(b):
+        return [lambda: V("i", vec.tensor_copy, T["rb%d" % b][:, 0:1], T.his[:, b:b + 1], deps=[arr("i%d" % b), t_io2]),
+                lambda: V("i", vec.transpose, T["iw%d" % b][:, 96:128], T["rb%d" % b][:, :])]
+
+    zeros("d0")
+    t_wn = V("a", vec.tensor_scalar, c("wn", 0), T.psa[:, 0:96], 0.0, 256.0, OP.is_lt, OP.mult, deps=[t_mm])
+
+    def consts():
+        V("t", vec.tensor_scalar, T.mk[:, :], T.t16[:, :], ic, None, OP.is_equal, deps=[t_io], free=True)
+        V("t", vec.tensor_scalar, T.rs[:, :], T.t16[:, :], 0.0, None, OP.is_gt, free=True)
+        V("t", vec.tensor_scalar, T.dd1[:, 1:12 * L:2], T.p18[:, :], ic, None, OP.add, free=True)
+        V("t", vec.memset, T.cc[:, 3:4], -64.0 * 256 * CAP, free=True)
+    t_zn = make_list(0, t_wn, consts, lambda t: None)
     for b in (1, 2):
-        win = "b%d" % (b - 1)
-        t_m = pick("a", "b%d" % b, 0, win, 128, mo(b - 1), 96, t_cc + [t_mo] + now())
-        t_lg = S("s2", T.lg[:, :], T.iot[:, 0:128].indirect(mo(b - 1)), AF.Copy)
-        t_st = score(b, "b%d" % b, t_m + [t_i1])
-        if b == 2:
-            ids_pick("iw1", 96, 32, "idp", T.ll[:, 2:4], [])
-        ps = T["ps%d" % b]
-        V("a", vec.tensor_scalar, T.wn[:, :], ps[:, 0:96], 0.0, 256.0, OP.is_lt, OP.mult, deps=[t_st])
-        V("b", vec.tensor_scalar, T.nw[:, :], ps[:, 0:96], 0.0, BIG, OP.is_ge, OP.mult)
-        t_zc = V("a", vec.tensor_tensor_scan, T.zc[:, :], T.wn[:, :], T.zz[:, :], 0.0, OP.add, OP.add)
-        t_nl = V("b", vec.tensor_tensor, T.nl[:, :], T.nw[:, :], T.lg[:, :], OP.add, deps=[t_lg])
-        t_kk = V("p", vec.tensor_scalar, T.kk[:, b:b + 1], T.zc[:, 95:96], 256.0 * CAP, None, OP.min, deps=[t_zc])
-        V("a", vec.tensor_tensor, T.xk[:, :], T.zc[:, :], T.nl[:, :], OP.add, deps=[t_nl])
-        t_y0 = V("a", vec.tensor_scalar, T.y0[:, 0:96], T.xk[:, :], hi[0], lo[0], OP.min, OP.max)
-        V("b", vec.tensor_scalar, T.y1[:, 0:96], T.xk[:, :], hi[1], lo[1], OP.min, OP.max)
-        t_a0 = S("s1", T.jk[:, 0:97], T.y0[:, 0:97], AF.Copy, accum_out=T.acc[:, 0:1], deps=[t_y0])
-        t_a1 = V("b", vec.tensor_reduce, T.acc[:, 1:2], T.y1[:, 0:97], AxisListType.X, OP.add)
-        t_lo = V("a", vec.tensor_scalar, T.lo[:, 2 * b:2 * b + 2], T.acc[:, 0:2], 127.0, 0.0, OP.min, OP.max, deps=[t_a0, t_a1])
-        send("k%d" % b, "kk", b, b + 1, [t_kk])
-        send("l%d" % b, "lo", 2 * b, 2 * b + 2, [t_lo])
-        if b == 1:
-            send("u2", "qb1", 0, 96, t_m)
-            t_w[2] = DMA(g.sync, "y", "lw2", T.wt2[:, :], T.w[:, 4096:6144], [t_lo])
-        t_ws = []
+        iota("sh", T["h%d" % b][:, 384:512], [[0, 128]], 0, 0)
+        iota("sh", T["rb%d" % b][:, :], [[0, 32]], 0, 0)
+        iota("sh", T["iw%d" % b][:, 96:128], [[0, 32]], 0, 0)
+    iota("sh", T.iw0[:, 0:96], [[1, 96]], rank * PL, 0)
+    t_io2 = iota("sh", T.idp[:, 0:128], [[1, 128]], T.rank_of(partners[0]) * PL, 0)
+    t_lw[1] = load_w(1, [left(0)])
+    t_v = DMA(g.sync, "y", "lv", T.vt[:, :], T.v[:, :])
 
-        def qv():
-            t_ws.append(V("q", vec.quantize_mx, T.qv[:, :], T.sv[:, :], T.vt[:, :], deps=[t_v]))
-        if b == 1:
-            together(prep(1), [lambda: t_ws.append(quant_w(1)), qv], ids_take(0, "iw0"))
-            t_qv = t_ws[1]
-            ids_pick("iw1", 0, 96, "iw0", mo(0), [t_mo])
-        else:
-            together(ids_send(2, "iw1"), prep(2), [None, None, None, lambda: t_ws.append(quant_w(2))])
-            ids_pick("iw2", 0, 96, "iw1", mo(1), [t_mo])
-        V("q", vec.tensor_scalar, T.ksb[:, b - 1:b], T.kk[:, b - 1:b], T.ko[:, b - 1:b], 1.0 / 256, OP.min, OP.mult)
-        t_r = expert(b, 128, [t_ws[0]] + t_r + [arr(f) for f in (("w0", "w1") if b == 1 else ()) + ("u%d" % b, "c%d" % b, "s%d" % b)], None)
-        t_e = V("a", vec.quantize_mx, T["qe%d" % b][:, :], T["se%d" % b][:, :], T["h%d" % b][:, :], deps=t_r)
-        m = merge_list(b)
-        if b == 1:
-            together(ids_take(1, "idp"), m[:2])
-        else:
-            m[0]()
-            m[1]()
+    p = prep(0, *t_zn)
+    p[0]()
+    t_g[1] = gauge(1, "q")
+    t_mm = MM("st", T.psa, ("g1", 0), ("b0", 0), t_g[1] + [t_qb, t_wn])
+    p[1]()
+    p[2]()
+    p[3]()
+    t_w = [quant_w(0, 0)]
+    t_fo = flags("fw0", 96, T.psa, [t_mm])
+    t_w.append(quant_w(0, 1))
+    p[4]()
+    t_w += [quant_w(0, 2), quant_w(0, 3)]
+    t_g[2] = gauge(2, "q")
+    zeros("d1", "b1")
+    m = merge_list(0)
+    t_r, t_e = expert(0, t_w, [arr("a0"), arr("b0"), arr("s0")], m)
+
+    t_qv = []
+    for b in range(L):
+        nxt = ("g%d" % (b + 1), 0) if b < 2 else ("v", 0)
+        t_se = MM("st", T.pse, nxt, ("e%d" % b, 0), [t_e, t_fo] + (t_g[b + 1] if b < 2 else t_qv))
+        off = ll(b)
+        t_cs = pick_s("b%d" % b, 96, "e%d" % b, off, 32, [t_e, t_fo, arr("l%d" % b)] + now("vq"))
+        t_cv = pick_v("c", "b%d" % b, 96, "e%d" % b, off, 32, [t_e, t_fo, arr("l%d" % b)] + now("vq"))
         t_mo = m[2]()
-        t_cc = pick("a", "b%d" % b, 96, "e%d" % b, 128, T.ll[:, 2 * b:2 * b + 2], 32, [t_e, t_i1, arr("l%d" % b)])
-        if b == 1:
-            send2([("c2", "qb1", 96, 128), ("s2", "sb1", 0, 128)], t_cc)
+        if b == 0:
+            t_new = S("s3", T.iw0[:, 96:128], T.idp[:, :].indirect(off), AF.Copy, deps=[t_io2])
+        if b < 2:
+            t_fe = flags("fe%d" % b, 128, T.pse, [t_se])
+        else:
+            t_fe = S("s2", T.fe2[:, :], T.pse[:, 0:128], AF.Copy, deps=[t_se])
+        nb = "b%d" % (b + 1) if b < 2 else "f"
+        t_ss = pick_s(nb, 0, "b%d" % b, mo(b), 96, [t_cs, t_mo])
+        t_sv = pick_v("c", nb, 0, "b%d" % b, mo(b), 96, [t_cv, t_mo])
+        t_fn = V("f", vec.tensor_copy, T["fw%d" % b][:, 96:128], T["fe%d" % b][:, :].indirect(off), deps=[t_fe])
+        if b == 2:
+            break
+        columns(b + 1, t_sv, t_ss)
+        t_wn = V("a", vec.tensor_copy, c("wn", b + 1), T["fw%d" % b][:, :].indirect(mo(b)), deps=[t_fn, t_fo, t_mo])
+        give = []
+        if b == 0:
+            def gap1():
+                row_numbers(0, [t_new, t_mo])
+                zeros("d2", "b2")
+        else:
+            take = take_numbers(1)
 
-    t_m = pick("a", "f", 0, "b2", 128, mo(2), 96, t_cc + [t_mo])
-    t_st = MM("st", T.pv, ("v", 0), ("f", 0), [t_qv, t_i1] + t_m)
-    DMA(g.sync, "y", "oc1", T.oc[:, 0:4 * PL], T.qf[:, 0:96].bitcast(dt.uint8), t_m[:1])
+            def gap1():
+                take[0]()
+                t_qv.append(V("q", vec.quantize_mx, T.qv[:, :], T.sv[:, :], T.vt[:, :], deps=[t_v], free=True))
+                take[1]()
+                row_numbers(1, now("vi") + [t_mo])
+        t_zn = make_list(b + 1, t_wn, gap1, lambda t: give.extend(give_numbers(b + 1, t)))
+        t_mm = MM("st", T.psa, ("g2", 0) if b == 0 else ("v", 0), ("b%d" % (b + 1), 0), (t_g[2] if b == 0 else t_qv) + [t_sv, t_ss, t_fo] + now("vq"))
+        p = prep(b + 1, *t_zn)
+        p[0]()
+        t_w = [quant_w(b + 1, 0)]
+        p[1]()
+        give[0]()
+        t_w.append(quant_w(b + 1, 1))
+        p[2]()
+        give[1]()
+        if b == 0:
+            t_lw[2] = load_w(2, [left(1)])
+        p[3]()
+        t_w += [quant_w(b + 1, 2), quant_w(b + 1, 3)]
+        if b == 0:
+            t_fo = flags("fw1", 96, T.psa, [t_mm])
+        else:
+            t_fo = V("f", vec.tensor_copy, T.fw2[:, 0:96], T.psa[:, 0:96], deps=[t_mm], free=True)
+        p[4]()
+        m = merge_list(b + 1)
+        t_r, t_e = expert(b + 1, t_w, t_r + [arr("%s%d" % (f, b + 1)) for f in "abs"], m)
+
+    t_y = V("a", vec.tensor_copy, T.yb[:, :], T.fw2[:, :].indirect(mo(2)), deps=[t_fn, t_fo, t_mo])
     for k in range(4):
-        DMA(g.scalar, "s", "oc2", T.osc[4 * k:4 * k + 4, 0:PL], T.sf[32 * k:32 * k + 4, 0:96], t_m[1:])
-    t_ks = V("q", vec.tensor_scalar, T.ksb[:, 2:3], T.kk[:, 2:3], T.ko[:, 2:3], 1.0 / 256, OP.min, OP.mult)
-    t_y = V("a", vec.tensor_copy, T.yb[:, :], T.pv[:, 0:96], deps=[t_st])
+        DMA(g.sync, "y", "oc2", T.osc[4 * k:4 * k + 4, 0:PL], T.sf[32 * k:32 * k + 4, 0:96], [t_ss])
+    DMA(g.scalar, "s", "oc1", T.oc[:, 0:4 * PL], T.qf[:, 0:96].bitcast(dt.uint8), [t_sv])
     DMA(g.sync, "y", "oy", T.y[:, :], T.yb[:, :], [t_y])
-    DMA(g.sync, "y", "oi", T.ks[0:1, :], T.ksb[0:1, :], [t_ks])
-    together(ids_take(2, "iw2"))
-    t_id = ids_pick("idl", 0, 96, "iw2", mo(2), [t_mo])
+    for f in take_numbers(2):
+        f()
+    t_id = S("s3", T.idl[:, :], T.iw2[:, :].indirect(mo(2)), AF.Copy, deps=now("vi"))
     DMA(g.scalar, "s", "oi", T.ids[0:1, :], T.idl[0:1, :], [t_id])
+    V("f", vec.tensor_tensor, T.km[:, :], T.zc[:, 95:96 * L:96], T.ko[:, :], OP.min, deps=now("va"))
+    t_ks = V("f", vec.tensor_scalar, T.ksb[:, :], T.km[:, :], 256.0 * CAP, 1.0 / 256, OP.min, OP.mult)
+    DMA(g.sync, "y", "ok", T.ks[0:1, :], T.ksb[0:1, :], [t_ks])
     need("g", g, [(s, n) for s, n in cnt.items() if n] + [arr(f) for f in FLOWS])

from concourse.bass import DstId, RemoteDMATransfer
from concourse.mybir import dt, AluOpType, ActivationFunctionType

PL, L, CAP = 96, 3, 32
OP, AF = AluOpType, ActivationFunctionType
F8, U8, F32, BF, U16, I32 = "float8_e4m3fn_x4", "uint8", "float32", "bfloat16", "uint16", "int32"
BIG = 16384.0

SCRATCH = {}


def _buf(name, n, dtype, where="sbuf"):
    SCRATCH[name] = (where, [128, n], dtype)


def _pair(name, n):
    _buf("q" + name, n, F8)
    _buf("s" + name, n, U8)


for _n, _w in (("xt", 512), ("ut", 512), ("vt", 512), ("zt", 512), ("wt0", 2048), ("wt1", 2048), ("wt2", 2048), ("h0", 512), ("h1", 512), ("h2", 512),
               ("zc", 96 * L)):
    _buf(_n, _w, BF)
for _n, _w in (("u", 128), ("g0", 128), ("g1", 128), ("g2", 128), ("w0", 512), ("w1", 512), ("w2", 512), ("v", 128),
               ("b0", 128), ("b1", 224), ("b2", 224), ("f", 96), ("d0", 224), ("d1", 224), ("d2", 224), ("e0", 128), ("e1", 128), ("e2", 128)):
    _pair(_n, _w)
for _n in ("psa", "pse", "pr0", "pr1", "pr2", "pr3"):
    _buf(_n, 512, F32, "psum")
for _n, _w in (("t16", 96), ("p18", 18), ("cc", 4), ("mk", 96), ("rs", 96), ("zz", 96), ("dd0", 12 * L), ("dd1", 12 * L), ("so", 12 * L),
               ("wn", 96 * L), ("nw", 96 * L), ("jk", 96 * L), ("jk2", 96 * L), ("acc", 2 * L), ("cw", 96 * L), ("dg", 96 * L),
               ("ds", 96 * L), ("t6", 6 * L), ("ov", 6 * L), ("dx", 6 * L), ("fe0", 128), ("fe1", 128), ("fe2", 128), ("fw0", 128), ("fw1", 128), ("fw2", 128),
               ("idp", 128), ("iw0", 128), ("iw1", 128), ("iw2", 128), ("idl", 96), ("si1", 32), ("si2", 32), ("sit1", 32), ("sit2", 32),
               ("rb1", 32), ("rb2", 32), ("km", 3), ("ksb", 3), ("yb", 96)):
    _buf(_n, _w, F32)
_buf("iq", 2, I32)
_buf("iqa", 2, I32)
_buf("cf", 8 * L, U16)
_buf("mo", 8 * L, U16)
_buf("lo", 2 * L, U16)
_buf("ll", 2 * L, U16)
_buf("ko", L, BF)
_buf("mine", L, U16)
_buf("his", L, U16)
for _b in range(L):
    _buf("xa%d" % _b, 48, F8)
    _buf("xb%d" % _b, 48, F8)
    _buf("xs%d" % _b, 96, U8)
_buf("xks", L, BF)
_buf("xis", L, U16)
_buf("xls", 2 * L, U16)

FLOWS = {}
for _b in range(L):
    FLOWS["a%d" % _b] = (0, _b, "xa%d" % _b, 0, "qd%d" % _b, 0, 48)
    FLOWS["b%d" % _b] = (2, _b, "xb%d" % _b, 0, "qd%d" % _b, 48, 48)
    FLOWS["s%d" % _b] = (1, _b, "xs%d" % _b, 0, "sd%d" % _b, 0, 96)
    FLOWS["k%d" % _b] = (0, _b, "xks", _b, "ko", _b, 1)
    FLOWS["l%d" % _b] = (0, _b, "xls", 2 * _b, "ll", 2 * _b, 2)
    if _b:
        FLOWS["i%d" % _b] = (1, _b, "xis", _b, "his", _b, 1)
ORDER = (("a0", "k0", "l0", "a1", "k1", "l1", "a2", "k2", "l2"), ("s0", "s1", "i1", "s2", "i2"), ("b0", "b1", "b2"))

VCH, SCH = ["va", "vc", "ve", "vf", "vp", "vi", "vq", "vk", "vm", "vt"], ["s1", "s2", "s3", "s4"]
SEMAPHORES = (["a_" + f for f in FLOWS] + VCH + SCH + ["st", "r0", "r1", "r2", "r3", "sq", "sg", "sh", "lsa", "ls0", "ls1", "ls2", "lx", "lu", "lv",
              "oy", "oc1", "oc2", "oi", "ok"] + ["lw%d%d" % (_b, _i) for _b in range(L) for _i in range(4)])


def _raw(view, name):
    return view.bitcast(dt.uint8) if SCRATCH[name][2] == F8 else view


def _mask(es):
    return sum(1 << e for e in es)


def _relays(core, T, topo):
    r = T.rank_of(core)
    ps = [T.cores[r ^ (1 << b)] for b in range(L)]
    rel = [c for c in topo.cores_of(core) if c != core and all(topo.may_write(c, p) for p in ps)]
    rel.sort(key=lambda c: (topo.die(c) != topo.die(core), c))
    return rel[:3], ps


def _hop1(f, src, dst, topo):
    es = topo.engines(src, dst)
    h = len(es) // 2
    return es[:h] if f[0] == "a" else es[h:] if f[0] == "b" else es


def _relay_program(g, core, me, partners, T, topo, rankcore):
    sent = 0
    for f in ORDER[me]:
        _, lev, xb, xa, db, a, w = FLOWS[f]
        g.wait_ge(T.sem["a_" + f], len(_hop1(f, rankcore, core, topo)))
        dst = partners[lev]
        rid, pid = topo.addr(dst, core)
        es = topo.engines(core, dst)
        g.remote_dma(_raw(T[db][:, a:a + w], db), _raw(T[xb][:, xa:xa + w], xb), T.sem["a_" + f], T.sem.lsa, pid, rid, _mask(es))
        sent += len(es)
    g.wait_ge(T.sem.lsa, sent)


def rank_program(g, core, T, topo):
    rank = T.rank_of(core)
    if rank is None:
        for rc in T.cores:
            if rc in topo.cores_of(core):
                rel, partners = _relays(rc, T, topo)
                if core in rel:
                    _relay_program(g, core, rel.index(core), partners, T, topo, rc)
        return
    rel, partners = _relays(core, T, topo)
    cnt = {}
    seen = {}
    vec = g.vector

    def need(q, eng, toks):
        best = {}
        for s, n in toks:
            if seen.get((q, s), 0) < n:
                best[s] = max(n, best.get(s, 0))
        for s in best:
            eng.wait_ge(T.sem[s], best[s])
            seen[(q, s)] = best[s]

    def bump(s, ins, n=1):
        ins.then_inc(T.sem[s], n)
        cnt[s] = cnt.get(s, 0) + n
        return (s, cnt[s])

    def now(*names):
        return [(s, cnt[s]) for s in (names or VCH + SCH) if cnt.get(s)]

    def V(ch, call, *args, deps=(), free=False, **kw):
        s = "v" + ch
        need("v", vec, list(deps) + ([] if free else now(s)))
        return bump(s, call(*args, **kw))

    def S(ch, *args, deps=(), **kw):
        need("s", g.scalar, list(deps) + now(ch))
        return bump(ch, g.scalar.activation(*args, **kw))

    def MM(s, out, l, r, deps):
        need("t", g.tensor, deps)
        (ln, la), (rn, ra) = l, r
        return bump(s, g.tensor.matmul_mx(out[:, 0:128], T["q" + ln][:, la:la + 128], T["s" + ln][:, la:la + 128],
                                          T["q" + rn][:, ra:ra + 128], T["s" + rn][:, ra:ra + 128], True, True))

    def DMA(eng, q, s, out, in_, deps=()):
        need(q, eng, deps)
        return bump(s, eng.dma_start(out, in_), 16)

    def pick_s(out, a, win, off, w, deps=()):
        return S("s1", T["s" + out][:, a:a + w], T["s" + win][:, 0:128].indirect(off), AF.Copy, deps=deps)

    def pick_v(ch, out, a, win, off, w, deps=()):
        return V(ch, vec.tensor_copy, T["q" + out][:, a:a + w].bitcast(dt.uint32), T["q" + win][:, 0:128].bitcast(dt.uint32).indirect(off), deps=deps)

    def hop1(f, name, a, b):
        k, _, xb, xa, _, _, w = FLOWS[f]
        rid, pid = topo.addr(rel[k], core)
        return rid, pid, _hop1(f, core, rel[k], topo), _raw(T[xb][:, xa:xa + w], xb), _raw(T[name][:, a:b], name)

    def left(b):
        return ("ls%d" % b, cnt["ls%d" % b])

    def send(f, name, a, b, deps):
        need("g", g, deps)
        rid, pid, es, out, in_ = hop1(f, name, a, b)
        ls = "ls%d" % FLOWS[f][1]
        g.remote_dma(out, in_, T.sem["a_" + f], T.sem[ls], pid, rid, _mask(es))
        cnt[ls] = cnt.get(ls, 0) + len(es)

    def send2(parts, deps):
        need("g", g, deps)
        tr = []
        for f, name, a, b in parts:
            rid, pid, es, out, in_ = hop1(f, name, a, b)
            ls = "ls%d" % FLOWS[f][1]
            tr.append(RemoteDMATransfer(dst_ids=[DstId(rid=rid, pnc=pid)], dma_engine_mask=_mask(es), remote_sem=T.sem["a_" + f], srcs=[in_], dsts=[out]))
            cnt[ls] = cnt.get(ls, 0) + len(es)
        g.remote_dma_fused(tr, local_sem=T.sem[ls])

    def arr(f):
        src = _relays(partners[FLOWS[f][1]], T, topo)[0][FLOWS[f][0]]
        return ("a_" + f, len(topo.engines(src, core)))

    def columns(b, tq, ts):
        send2([("a%d" % b, "qb%d" % b, 0, 48), ("b%d" % b, "qb%d" % b, 48, 96)], [tq])
        send("s%d" % b, "sb%d" % b, 0, 96, [ts])

    def c(name, b, w=PL):
        return T[name][:, w * b:w * b + w]

    def mo(b):
        return T.mo[:, 8 * b:8 * b + 6]

    def ll(b):
        return T.ll[:, 2 * b:2 * b + 2]

    t_u = DMA(g.sync, "y", "lu", T.ut[:, 0:16], T.u[:, 0:16])
    t_x = DMA(g.scalar, "s", "lx", T.xt[:, 0:4 * PL], T.x[:, 0:4 * PL])

    def load_w(b, deps=()):
        return [DMA(g.sync, "y", "lw%d%d" % (b, i), T["wt%d" % b][:, 512 * i:512 * i + 512], T.w[:, 2048 * b + 512 * i:2048 * b + 512 * i + 512], deps)
                for i in range(4)]
    t_lw = [load_w(0), None, None]

    def iota(s, view, pattern, base, cm):
        return bump(s, g.iota(view, pattern, base, cm, allow_small_or_imprecise_dtypes=True))
    t_iq = bump("sq", g.iota(T.iq[:, 0:2], [[0, 2]], 0, 1))
    iota("sg", T.t16[:, 0:96], [[0, 6], [1, 16]], 0, 0)
    t_io = iota("sg", T.p18[:, 0:18], [[0, 3], [16, 6]], 0, 0)

    V("k", vec.memset, T.ut[:, 16:512], 0.0, free=True)
    V("k", vec.memset, T.cf[:, 0:8], 0, free=True)
    V("k", vec.memset, T.xt[:, 384:512], 0.0, free=True)
    V("k", vec.memset, T.zz[:, :], 0.0, free=True)
    t_k = now("vk")
    ic, jb0, jb1 = T.cc[:, 0:1], T.cc[:, 1:2], T.cc[:, 2:3]
    V("c", vec.tensor_scalar, T.iqa[:, :], T.iq[:, :], 15, None, OP.bitwise_and, deps=[t_iq])
    V("k", vec.memset, T.zt[:, :], 0.0, free=True)
    t_ic = V("c", vec.tensor_copy, ic, T.iqa[:, 0:1])
    V("k", vec.memset, T.cf[:, 8:16], 1, free=True)
    V("k", vec.memset, T.cf[:, 16:24], 2, free=True)
    V("t", vec.tensor_scalar, jb0, ic, 256.0, 128.0, OP.mult, OP.add, deps=[t_ic])
    t_jc = V("t", vec.tensor_scalar, jb1, ic, 256.0, 4224.0, OP.mult, OP.add, free=True)
    V("k", vec.memset, T.dd0[:, :], 0.0, free=True)
    V("k", vec.memset, T.h0[:, 384:512], 0.0, free=True)
    t_qu = V("a", vec.quantize_mx, T.qu[:, :], T.su[:, :], T.ut[:, :], deps=[t_u] + t_k)
    t_qb = V("q", vec.quantize_mx, T.qb0[:, :], T.sb0[:, :], T.xt[:, :], deps=[t_x])

    def gauge(b, ch):
        off = T.cf[:, 8 * b:8 * b + 8]
        s = pick_s("g%d" % b, 0, "u", off, 128, [t_qu] + now("vk"))
        return [pick_v(ch, "g%d" % b, 0, "u", off, 128, [t_qu] + now("vk")), s]
    t_g = [gauge(0, "a"), None, None]
    columns(0, t_qb, t_qb)
    t_mm = MM("st", T.psa, ("g0", 0), ("b0", 0), t_g[0] + [t_qb])

    def zeros(*names):
        for n in names:
            V("q", vec.quantize_mx, T["q" + n][:, 96:224], T["s" + n][:, 96:224], T.zt[:, :], deps=now("vk"), free=True)

    def make_list(b, t_wn, gap1, gap2):
        t_zc = V("a", vec.tensor_tensor_scan, c("zc", b), c("wn", b), T.zz[:, :], 0.0, OP.add, OP.add)
        a0 = S("s2", c("jk", b), c("zc", b), AF.Sign, bias=jb0, scale=-1.0, accum_out=T.acc[:, 2 * b:2 * b + 1], deps=[t_zc, t_jc])
        a1 = S("s3", c("jk2", b), c("zc", b), AF.Sign, bias=jb1, scale=-1.0, accum_out=T.acc[:, 2 * b + 1:2 * b + 2])
        t_nw = S("s4", c("nw", b), c("wn", b), AF.Identity, bias=BIG, scale=-BIG / 256, deps=[t_wn])
        send("k%d" % b, "zc", 96 * b + 95, 96 * b + 96, [t_zc])
        gap1()
        t_lo = V("a", vec.tensor_scalar, T.lo[:, 2 * b:2 * b + 2], T.acc[:, 2 * b:2 * b + 2], 96.0, 0.5, OP.add, OP.mult, deps=[a0, a1])
        send("l%d" % b, "lo", 2 * b, 2 * b + 2, [t_lo])
        gap2(t_lo)
        return t_zc, t_nw

    def prep(b, t_zc, t_nw):
        ds, d1 = T.ds[:, 96 * b + 15:96 * b + 96:16], T.dd1[:, 12 * b:12 * b + 12:2]
        t = []

        def small():
            d = now("vp")
            t.append(S("s4", c("t6", b, 6), ds, AF.Identity, bias=PL - 1.0, scale=1.0 / 256, deps=d))
            t.append(S("s2", c("ov", b, 6), ds, AF.Relu, scale=64.0, bias=T.cc[:, 3:4], deps=d + now("vt")))

        def last():
            V("p", vec.tensor_tensor, d1, c("t6", b, 6), T.dd1[:, 12 * b + 1:12 * b + 12:2], OP.subtract, deps=t[:1])
            V("p", vec.tensor_tensor, c("dx", b, 6), c("ov", b, 6), ds, OP.add, deps=t[1:], free=True)
        return [lambda: V("p", vec.tensor_tensor, c("cw", b), c("zc", b), c("nw", b), OP.add, deps=[t_zc, t_nw]),
                lambda: V("p", vec.tensor_tensor, c("dg", b), c("cw", b), T.mk[:, :], OP.mult, deps=now("vt")),
                lambda: V("p", vec.tensor_tensor_scan, c("ds", b), T.rs[:, :], c("dg", b), 0.0, OP.mult, OP.add),
                small, last]

    def merge_list(b):
        return [lambda: V("m", vec.tensor_scalar, T.dd0[:, 12 * b + 1:12 * b + 12:2], c("dx", b, 6), T.ko[:, b:b + 1], None, OP.is_le,
                          deps=[arr("k%d" % b)] + now("vp", "vk")),
                lambda: V("m", vec.tensor_tensor_scan, c("so", b, 12), c("dd0", b, 12), c("dd1", b, 12), 0.0, OP.mult, OP.add),
                lambda: V("m", vec.tensor_copy, T.mo[:, 8 * b:8 * b + 6], T.so[:, 12 * b + 1:12 * b + 12:2])]

    def quant_w(b, i):
        return V("q", vec.quantize_mx, T["qw%d" % b][:, 128 * i:128 * i + 128], T["sw%d" % b][:, 128 * i:128 * i + 128],
                 T["wt%d" % b][:, 512 * i:512 * i + 512], deps=[t_lw[b][i]], free=True)

    def expert(b, tw, deps, m):
        h, n = T["h%d" % b], PL
        tr = [MM("r%d" % i, T["pr%d" % i], ("w%d" % b, 128 * i), ("d%d" % b, 0), deps + [tw[i]]) for i in range(4)]
        t0 = S("s1", h[:, 0:4 * n:4], T.pr0[:, 0:n], AF.Copy, scale=0.0625, deps=[tr[0]])
        t2 = S("s2", h[:, 2:4 * n:4], T.pr2[:, 0:n], AF.Copy, scale=0.0625, deps=[tr[2]])
        t1 = V("e", vec.tensor_scalar, h[:, 1:4 * n:4], T.pr1[:, 0:n], 0.0625, None, OP.mult, deps=[tr[1]], free=True)
        t3 = V("e", vec.tensor_scalar, h[:, 3:4 * n:4], T.pr3[:, 0:n], 0.0625, None, OP.mult, deps=[tr[3]], free=True)
        t_r = [t0, t1, t2, t3]
        t_e = V("e", vec.quantize_mx, T["qe%d" % b][:, :], T["se%d" % b][:, :], T["h%d" % b][:, :], deps=t_r + [t_io2] + now("vk"))
        m[0]()
        m[1]()
        return t_r, t_e

    def flags(buf, n, ps, deps):
        return V("f", vec.tensor_scalar, T[buf][:, 0:n], ps[:, 0:n], 0.0, 256.0, OP.is_lt, OP.mult, deps=deps, free=True)

    def row_numbers(b, deps):
        return S("s3", T["iw%d" % (b + 1)][:, 0:96], T["iw%d" % b][:, :].indirect(mo(b)), AF.Copy, deps=deps)

    def give_numbers(b, t_lo):
        t = S("s3", T["si%d" % b][:, :], T["iw%d" % b][:, :].indirect(T.lo[:, 2 * b:2 * b + 2]), AF.Copy, deps=[t_lo])

        def out():
            send("i%d" % b, "mine", b, b + 1, [V("i", vec.tensor_copy, T.mine[:, b:b + 1], T["sit%d" % b][:, 0:1])])
        return [lambda: V("i", vec.transpose, T["sit%d" % b][:, :], T["si%d" % b][:, :], deps=[t]), out]

    def take_numbers(b):
        return [lambda: V("i", vec.tensor_copy, T["rb%d" % b][:, 0:1], T.his[:, b:b + 1], deps=[arr("i%d" % b), t_io2]),
                lambda: V("i", vec.transpose, T["iw%d" % b][:, 96:128], T["rb%d" % b][:, :])]

    zeros("d0")
    t_wn = V("a", vec.tensor_scalar, c("wn", 0), T.psa[:, 0:96], 0.0, 256.0, OP.is_lt, OP.mult, deps=[t_mm])

    def consts():
        V("t", vec.tensor_scalar, T.mk[:, :], T.t16[:, :], ic, None, OP.is_equal, deps=[t_io], free=True)
        V("t", vec.tensor_scalar, T.rs[:, :], T.t16[:, :], 0.0, None, OP.is_gt, free=True)
        V("t", vec.tensor_scalar, T.dd1[:, 1:12 * L:2], T.p18[:, :], ic, None, OP.add, free=True)
        V("t", vec.memset, T.cc[:, 3:4], -64.0 * 256 * CAP, free=True)
    t_zn = make_list(0, t_wn, consts, lambda t: None)
    for b in (1, 2):
        iota("sh", T["h%d" % b][:, 384:512], [[0, 128]], 0, 0)
        iota("sh", T["rb%d" % b][:, :], [[0, 32]], 0, 0)
        iota("sh", T["iw%d" % b][:, 96:128], [[0, 32]], 0, 0)
    iota("sh", T.iw0[:, 0:96], [[1, 96]], rank * PL, 0)
    t_io2 = iota("sh", T.idp[:, 0:128], [[1, 128]], T.rank_of(partners[0]) * PL, 0)
    t_lw[1] = load_w(1, [left(0)])
    t_v = DMA(g.sync, "y", "lv", T.vt[:, :], T.v[:, :])

    p = prep(0, *t_zn)
    p[0]()
    t_g[1] = gauge(1, "q")
    t_mm = MM("st", T.psa, ("g1", 0), ("b0", 0), t_g[1] + [t_qb, t_wn])
    p[1]()
    p[2]()
    p[3]()
    t_w = [quant_w(0, 0)]
    t_fo = flags("fw0", 96, T.psa, [t_mm])
    t_w.append(quant_w(0, 1))
    p[4]()
    t_w += [quant_w(0, 2), quant_w(0, 3)]
    t_g[2] = gauge(2, "q")
    zeros("d1", "b1")
    m = merge_list(0)
    t_r, t_e = expert(0, t_w, [arr("a0"), arr("b0"), arr("s0")], m)

    t_qv = []
    for b in range(L):
        nxt = ("g%d" % (b + 1), 0) if b < 2 else ("v", 0)
        t_se = MM("st", T.pse, nxt, ("e%d" % b, 0), [t_e, t_fo] + (t_g[b + 1] if b < 2 else t_qv))
        off = ll(b)
        t_cs = pick_s("b%d" % b, 96, "e%d" % b, off, 32, [t_e, t_fo, arr("l%d" % b)] + now("vq"))
        t_cv = pick_v("c", "b%d" % b, 96, "e%d" % b, off, 32, [t_e, t_fo, arr("l%d" % b)] + now("vq"))
        t_mo = m[2]()
        if b == 0:
            t_new = S("s3", T.iw0[:, 96:128], T.idp[:, :].indirect(off), AF.Copy, deps=[t_io2])
        if b < 2:
            t_fe = flags("fe%d" % b, 128, T.pse, [t_se])
        else:
            t_fe = S("s2", T.fe2[:, :], T.pse[:, 0:128], AF.Copy, deps=[t_se])
        nb = "b%d" % (b + 1) if b < 2 else "f"
        t_ss = pick_s(nb, 0, "b%d" % b, mo(b), 96, [t_cs, t_mo])
        t_sv = pick_v("c", nb, 0, "b%d" % b, mo(b), 96, [t_cv, t_mo])
        t_fn = V("f", vec.tensor_copy, T["fw%d" % b][:, 96:128], T["fe%d" % b][:, :].indirect(off), deps=[t_fe])
        if b == 2:
            break
        columns(b + 1, t_sv, t_ss)
        t_wn = V("a", vec.tensor_copy, c("wn", b + 1), T["fw%d" % b][:, :].indirect(mo(b)), deps=[t_fn, t_fo, t_mo])
        give = []
        if b == 0:
            def gap1():
                row_numbers(0, [t_new, t_mo])
                zeros("d2", "b2")
        else:
            take = take_numbers(1)

            def gap1():
                take[0]()
                t_qv.append(V("q", vec.quantize_mx, T.qv[:, :], T.sv[:, :], T.vt[:, :], deps=[t_v], free=True))
                take[1]()
                row_numbers(1, now("vi") + [t_mo])
        t_zn = make_list(b + 1, t_wn, gap1, lambda t: give.extend(give_numbers(b + 1, t)))
        t_mm = MM("st", T.psa, ("g2", 0) if b == 0 else ("v", 0), ("b%d" % (b + 1), 0), (t_g[2] if b == 0 else t_qv) + [t_sv, t_ss, t_fo] + now("vq"))
        p = prep(b + 1, *t_zn)
        p[0]()
        t_w = [quant_w(b + 1, 0)]
        p[1]()
        give[0]()
        t_w.append(quant_w(b + 1, 1))
        p[2]()
        give[1]()
        if b == 0:
            t_lw[2] = load_w(2, [left(1)])
        p[3]()
        t_w += [quant_w(b + 1, 2), quant_w(b + 1, 3)]
        if b == 0:
            t_fo = flags("fw1", 96, T.psa, [t_mm])
        else:
            t_fo = V("f", vec.tensor_copy, T.fw2[:, 0:96], T.psa[:, 0:96], deps=[t_mm], free=True)
        p[4]()
        m = merge_list(b + 1)
        t_r, t_e = expert(b + 1, t_w, t_r + [arr("%s%d" % (f, b + 1)) for f in "abs"], m)

    t_y = V("a", vec.tensor_copy, T.yb[:, :], T.fw2[:, :].indirect(mo(2)), deps=[t_fn, t_fo, t_mo])
    for k in range(4):
        DMA(g.sync, "y", "oc2", T.osc[4 * k:4 * k + 4, 0:PL], T.sf[32 * k:32 * k + 4, 0:96], [t_ss])
    DMA(g.scalar, "s", "oc1", T.oc[:, 0:4 * PL], T.qf[:, 0:96].bitcast(dt.uint8), [t_sv])
    DMA(g.sync, "y", "oy", T.y[:, :], T.yb[:, :], [t_y])
    for f in take_numbers(2):
        f()
    t_id = S("s3", T.idl[:, :], T.iw2[:, :].indirect(mo(2)), AF.Copy, deps=now("vi"))
    DMA(g.scalar, "s", "oi", T.ids[0:1, :], T.idl[0:1, :], [t_id])
    V("f", vec.tensor_tensor, T.km[:, :], T.zc[:, 95:96 * L:96], T.ko[:, :], OP.min, deps=now("va"))
    t_ks = V("f", vec.tensor_scalar, T.ksb[:, :], T.km[:, :], 256.0 * CAP, 1.0 / 256, OP.min, OP.mult)
    DMA(g.sync, "y", "ok", T.ks[0:1, :], T.ksb[0:1, :], [t_ks])
    need("g", g, [(s, n) for s, n in cnt.items() if n] + [arr(f) for f in FLOWS])
